import numpy as np
import ml_dtypes


def mxq(x, axis, fmt="e4m3"):
    dtype, down = {"e4m3": (ml_dtypes.float8_e4m3fn, 7), "e5m2": (ml_dtypes.float8_e5m2, 14)}[fmt]
    v = np.moveaxis(np.asarray(x, np.float32).astype(ml_dtypes.bfloat16).astype(np.float64), axis, -1)
    blocks = v.reshape(v.shape[:-1] + (-1, 32))
    amax = np.abs(blocks).max(-1, keepdims=True)
    byte = np.maximum(np.where(amax > 0, np.frexp(amax)[1] - 1 + 127, 0) - down, 1)
    scale = np.exp2(byte - 127.0)
    codes = (blocks / scale).astype(np.float32).astype(dtype).astype(np.float64)
    return np.moveaxis((codes * scale).reshape(v.shape), -1, axis)


WIDE = False


def mx_kscale(k):
    if not WIDE:
        return np.ones(k)
    levels = np.array([10, -10, 5, -5, 0])
    if k % 512:
        return np.exp2(np.random.permutation(np.resize(levels, k // 32))).repeat(32)
    a = np.empty((k // 512, 16))
    for p in range(k // 512):
        a[p, :8] = np.random.permutation(np.resize(levels, 8))
        for g in range(8):
            far = levels[np.abs(levels - a[p, g]) >= 10]
            a[p, g + 8] = far[np.random.randint(len(far))]
    return np.exp2(a.ravel()).repeat(32)


BF16 = ml_dtypes.bfloat16


def bf(x):
    return np.asarray(x, np.float32).astype(BF16)


def f64(x):
    return np.asarray(x).astype(np.float64)


E2M1 = np.array([0.0, 0.5, 1.0, 1.5, 2.0, 3.0, 4.0, 6.0, -0.0, -0.5, -1.0, -1.5, -2.0, -3.0, -4.0, -6.0])


def pack_weight(w, fmt):
    k, n = w.shape
    w = f64(bf(w)).reshape(k // 32, 32, n)
    amax = np.abs(w).max(1)
    if fmt == "e4m3":
        byte = np.frexp(amax)[1] - 1 + 127 - 7
    else:
        mant, ex = np.frexp(amax / 6.0)
        byte = np.where(mant > 0.5, ex, ex - 1) + 127
    byte = np.clip(np.where(amax > 0, byte, 1), 1, 254)
    scaled = (w * np.exp2(127.0 - byte)[:, None, :]).reshape(k, n).astype(np.float32)
    by_word = np.ascontiguousarray(scaled.reshape(k // 512, 128, 4, n).transpose(0, 1, 3, 2))
    if fmt == "e4m3":
        words = by_word.astype(ml_dtypes.float8_e4m3fn).view(np.uint8)
    else:
        c = by_word.astype(ml_dtypes.float4_e2m1fn).view(np.uint8) & 0xF
        words = c[..., 0::2] | (c[..., 1::2] << 4)
    return np.ascontiguousarray(words), np.ascontiguousarray(byte.astype(np.uint8).reshape(k // 512, 16, n))


def unpack_weight(words, scales, fmt):
    g, p, n, _ = words.shape
    if fmt == "e4m3":
        vals = np.ascontiguousarray(words).view(ml_dtypes.float8_e4m3fn).astype(np.float64)
    else:
        nib = np.empty((g, p, n, 4), np.uint8)
        nib[..., 0::2] = words & 0xF
        nib[..., 1::2] = words >> 4
        vals = E2M1[nib]
    vals = vals * np.repeat(np.exp2(scales.astype(np.float64) - 127.0), 8, axis=1)[..., None]
    return vals.transpose(0, 1, 3, 2).reshape(g * 512, n)
def pack4(w):
    words, scales = pack_weight(w, "e2m1")
    return words.reshape(words.shape[0], 128, -1), scales


def unpack4(words, scales):
    return unpack_weight(words.reshape(words.shape[0], 128, -1, 2), scales, "e2m1")


M, H, F, D, V, R = 1024, 1024, 2048, 1024, 1024, 512


def draw0():
    sa = mx_kscale(H)
    sm = mx_kscale(F)
    t = mx_kscale(D)
    u = mx_kscale(M)
    attn = bf(np.random.standard_normal((M, H)) * sa * u[:, None])
    wo = bf(np.random.standard_normal((H, D)) / np.sqrt(H) / sa[:, None] * t)
    mlp = bf(np.random.standard_normal((M, F)) * sm * u[:, None])
    wd = bf(np.random.standard_normal((F, D)) / np.sqrt(F) / sm[:, None] * t)
    resid = bf(np.random.standard_normal((M, D)) * u[:, None] * t)
    wp_words, wp_scales = pack4(np.random.standard_normal((D, V)) / np.sqrt(D) / t[:, None])
    pool = bf(np.random.standard_normal((R, M)) / np.sqrt(M) / u)
    return {"attn": attn, "wo": wo, "mlp": mlp, "wd": wd, "resid": resid,
            "wp_words": wp_words, "wp_scales": wp_scales, "pool": pool}


def core(attn, wo, mlp, wd, resid, wp_words, wp_scales, pool):
    a = mxq(f64(attn), 1, "e4m3") @ mxq(f64(wo), 0, "e4m3")
    m = mxq(f64(mlp), 1, "e4m3") @ mxq(f64(wd), 0, "e4m3")
    h = f64(resid) + a + m
    y = mxq(h, 1, "e4m3") @ unpack4(wp_words, wp_scales)
    c = mxq(f64(pool), 1, "e4m3") @ mxq(h, 0, "e4m3")
    return y, c


def e4m3fn_bytes(y):
    return np.clip(np.asarray(y, np.float64), -448.0, 448.0).astype(np.float32).astype(ml_dtypes.float8_e4m3fn).view(np.uint8)


def e4m3fn_values(b):
    return np.asarray(b, np.uint8).view(ml_dtypes.float8_e4m3fn).astype(np.float64)


def setup_inputs():
    d = draw0()
    x0 = np.asarray(d['pool']).astype(np.float64)
    s = (np.max(np.abs(x0), axis=(0,), keepdims=True) / 448.0).astype(np.float32)
    out = {}
    for k, v in d.items():
        if k == 'pool':
            out['pool_bytes'] = e4m3fn_bytes(x0 / s.astype(np.float64))
            out['pool_scale'] = s
        else:
            out[k] = v
    return out


def reference(attn, wo, mlp, wd, resid, wp_words, wp_scales, pool_bytes, pool_scale):
    return core(attn, wo, mlp, wd, resid, wp_words, wp_scales, e4m3fn_values(pool_bytes) * pool_scale.astype(np.float64))

@@ -1,0 +1,402 @@
+from contextlib import ExitStack
+
+import concourse.mybir as mybir
+from concourse.masks import make_identity
+
+F32 = mybir.dt.float32
+BF16 = mybir.dt.bfloat16
+U32 = mybir.dt.uint32
+I32 = mybir.dt.int32
+U8 = mybir.dt.uint8
+FP8 = mybir.dt.float8_e4m3fn
+FP8X4 = mybir.dt.float8_e4m3fn_x4
+FP4X4 = mybir.dt.float4_e2m1fn_x4
+ADD = mybir.AluOpType.add
+MULT = mybir.AluOpType.mult
+
+P = 128
+M, H, F, D, V, R = 1024, 1024, 2048, 1024, 1024, 512
+FLOPS = 2 * M * D * (H + F) + 2 * M * D * V + 2 * R * M * D
+
+HALF = 512
+KA, KM = H // 512, F // 512
+PASSES = KA + KM
+V_COLS = 320
+
+
+def tile_two_writer_residual_s8_kernel(
+    tc, attn, wo, mlp, wd, resid, wp_words, wp_scales, pool_bytes, pool_scale, out_0, out_1
+):
+    nc = tc.nc
+    with ExitStack() as ctx:
+        keep = ctx.enter_context(tc.tile_pool(name="keep", bufs=1))
+        ring = ctx.enter_context(tc.tile_pool(name="ring", bufs=2))
+        psum = ctx.enter_context(tc.psum_pool(name="psum", bufs=4))
+
+        def kept(label, shape, dtype):
+            return keep.tile(shape, dtype, name=label, tag=label, bufs=1, align_bytes=64)
+
+        ident = kept("ident", [P, P], F32)
+        wp_sc = kept("wp_sc", [P, 2, V], U8)
+        make_identity(nc, ident[:])
+        nc.gpsimd.memset(wp_sc[:].rearrange("p g n -> p (g n)").bitcast(I32), 0)
+
+        ctx.enter_context(tc.manual_schedule())
+
+        attn_v = attn.rearrange("(g p t) k -> g p t k", p=P, t=4)
+        mlp_v = mlp.rearrange("(g p t) k -> g p t k", p=P, t=4)
+        resid_v = resid.rearrange("(g p t) d -> g p t d", p=P, t=4)
+        wo_v = wo.rearrange("(k p j) d -> k p j d", p=P, j=4)
+        wd_v = wd.rearrange("(k p j) d -> k p j d", p=P, j=4)
+        y_v = out_0.rearrange("(g p t) v -> g t p v", p=P, t=4)
+        c_v = out_1.rearrange("(p j) d -> j p d", j=4)
+
+        act_raw, act_grp, act_q = {}, {}, {}
+        w_raw, w_grp, w_q = {}, {}, {}
+        res, acc, h, ht_grp, ht_q, hc_grp, hc_q = {}, {}, {}, {}, {}, {}, {}
+        pl_val, pl_grp, pl_q = {}, {}, {}
+
+        def load_act(g, s, b):
+            x = ring.tile([P, 2, 1024], BF16, name=f"act{g}{s}{b}", tag="act", bufs=6, align_bytes=64)
+            two = slice(2 * b, 2 * b + 2)
+            if s == 0:
+                nc.sync.dma_start(out=x[:], in_=attn_v[g][:, two, :])
+            else:
+                nc.sync.dma_start(out=x[:], in_=mlp_v[g][:, two, 1024 * (s - 1) : 1024 * s])
+            act_raw[g, s, b] = x
+
+        def load_w(n, k):
+            x = ring.tile([P, 4, HALF], BF16, name=f"w{n}{k}", tag="wraw", bufs=5, align_bytes=64)
+            rows = wo_v[k] if k < KA else wd_v[k - KA]
+            nc.sync.dma_start(out=x[:], in_=rows[:, :, HALF * n : HALF * (n + 1)])
+            w_raw[n, k] = x
+
+        def load_res(g, n):
+            res[g, n] = kept(f"res{g}{n}", [P, 4, HALF], BF16)
+            nc.sync.dma_start(out=res[g, n][:], in_=resid_v[g][:, :, HALF * n : HALF * (n + 1)])
+
+        def turn_act(g, k, b):
+            bank = psum.tile([P, 4, P], F32, name=f"tr{g}{k}{b}", tag="tr", bufs=4)
+            words = act_raw[g, k // 2, b][:].rearrange("p t c -> p (t c)").bitcast(F32)
+            for t in range(2):
+                for u in range(2):
+                    first = 512 * t + 256 * (k % 2) + u
+                    nc.tensor.transpose(bank[:, 2 * t + u, :], words[:, first : first + 255 : 2], ident[:])
+            if (g, k) not in act_grp:
+                act_grp[g, k] = ring.tile([P, 512, 4], BF16, name=f"ag{g}{k}", tag="grp", bufs=6, align_bytes=64)
+            dst = act_grp[g, k][:].rearrange("p r j -> p (r j)").bitcast(F32)
+            nc.scalar.copy(
+                out=dst[:, 512 * b : 512 * (b + 1)].rearrange("p (t r u) -> p t r u", t=2, u=2),
+                in_=bank[:].rearrange("p (t u) r -> p t r u", u=2),
+            )
+
+        def quantize(label, grp):
+            codes = kept(label + "_c", [P, 512], U32)
+            scales = kept(label + "_s", [P, 512], U8)
+            nc.vector.quantize_mx(
+                out=codes[:].bitcast(FP8X4), scales=scales[:], in_=grp[:].rearrange("p c j -> p (c j)")
+            )
+            return codes, scales
+
+        def quant_act(g, k):
+            act_q[g, k] = quantize(f"aq{g}{k}", act_grp[g, k])
+
+        def interleave(label, src):
+            x = ring.tile([P, 512, 4], BF16, name=label, tag="wgrp", bufs=3, align_bytes=64)
+            for copy, lo, hi in ((nc.vector.tensor_copy, 0, V_COLS), (nc.scalar.copy, V_COLS, 512)):
+                copy(
+                    out=x[:, lo:hi, :].rearrange("p (c i) j -> p c j i", i=4),
+                    in_=src[:, :, lo:hi].rearrange("p j (c i) -> p c j i", i=4),
+                )
+            return x
+
+        def group_w(n, k):
+            w_grp[n, k] = interleave(f"wg{n}{k}", w_raw[n, k])
+
+        def quant_w(n, k):
+            w_q[n, k] = quantize(f"wq{n}{k}", w_grp[n, k])
+
+        def mx(out, a, b, start, stop):
+            nc.tensor.matmul_mx(
+                out=out, lhsT=a[0], lhsT_scale=a[1], rhs=b[0], rhs_scale=b[1], start=start, stop=stop
+            )
+
+        def stationary(q, t):
+            cols = slice(P * t, P * (t + 1))
+            return q[0][:, cols].bitcast(FP8X4), q[1][:, cols]
+
+        def moving(q):
+            return q[0][:].bitcast(FP8X4), q[1][:]
+
+        def write_stream(g, n, k, t):
+            if k == 0:
+                acc[g, n, t] = psum.tile([P, HALF], F32, name=f"acc{g}{n}{t}", tag="acc", bufs=4)
+            mx(acc[g, n, t][:], stationary(act_q[g, k], t), moving(w_q[n, k]), k == 0, k == PASSES - 1)
+
+        def add_res(g, n, t):
+            if t == 0:
+                h[g, n] = ring.tile([P, 4, HALF], BF16, name=f"h{g}{n}", tag="h", bufs=4, align_bytes=64)
+            nc.vector.tensor_tensor(
+                out=h[g, n][:, t, :].rearrange("p (u k e) -> p u k e", u=2, e=2),
+                in0=acc[g, n, t][:].rearrange("p (k u e) -> p u k e", u=2, e=2),
+                in1=res[g, n][:, t, :].rearrange("p (k u e) -> p u k e", u=2, e=2),
+                op=ADD,
+            )
+
+        def turn_h(g, n, b):
+            bank = psum.tile([P, 4, P], F32, name=f"ht{g}{n}{b}", tag="tr", bufs=4)
+            words = h[g, n][:].rearrange("p t c -> p (t c)").bitcast(F32)
+            for t in range(2):
+                for u in range(2):
+                    first = 256 * (2 * b + t) + P * u
+                    nc.tensor.transpose(bank[:, 2 * t + u, :], words[:, first : first + P], ident[:])
+            if b == 0:
+                ht_grp[g, n] = ring.tile([P, 512, 4], BF16, name=f"hg{g}{n}", tag="grp", bufs=6, align_bytes=64)
+            dst = ht_grp[g, n][:].rearrange("p r j -> p (r j)").bitcast(F32)
+            nc.scalar.copy(
+                out=dst[:, 512 * b : 512 * (b + 1)].rearrange("p (t r u) -> p t r u", t=2, u=2),
+                in_=bank[:].rearrange("p (t u) r -> p t r u", u=2),
+            )
+
+        def quant_ht(g, n):
+            ht_q[g, n] = quantize(f"hq{g}{n}", ht_grp[g, n])
+
+        def group_hc(g, n):
+            hc_grp[g, n] = interleave(f"hcg{g}{n}", h[g, n])
+
+        def quant_hc(g, n):
+            hc_q[g, n] = quantize(f"hcq{g}{n}", hc_grp[g, n])
+
+        def scale_pool(j):
+            if j % 2 == 0:
+                pl_val[j // 2] = ring.tile([P, 2, M], BF16, name=f"pv{j}", tag="act", bufs=6, align_bytes=64)
+            nc.vector.tensor_tensor(
+                out=pl_val[j // 2][:, j % 2, :], in0=pl_raw[:, j, :].bitcast(FP8), in1=pl_scale[:], op=MULT
+            )
+
+        def turn_pool(k, b):
+            bank = psum.tile([P, 4, P], F32, name=f"pt{k}{b}", tag="tr", bufs=4)
+            words = pl_val[b][:].rearrange("p j c -> p (j c)").bitcast(F32)
+            for t in range(2):
+                for u in range(2):
+                    first = 512 * t + 256 * k + u
+                    nc.tensor.transpose(bank[:, 2 * t + u, :], words[:, first : first + 255 : 2], ident[:])
+            if b == 0:
+                pl_grp[k] = ring.tile([P, 512, 4], BF16, name=f"pg{k}", tag="grp", bufs=6, align_bytes=64)
+            dst = pl_grp[k][:].rearrange("p r j -> p (r j)").bitcast(F32)
+            nc.scalar.copy(
+                out=dst[:, 512 * b : 512 * (b + 1)].rearrange("p (t r u) -> p t r u", t=2, u=2),
+                in_=bank[:].rearrange("p (t u) r -> p t r u", u=2),
+            )
+
+        def quant_pool(k):
+            pl_q[k] = quantize(f"pq{k}", pl_grp[k])
+
+        def project(g, t, engines):
+            x = ring.tile([P, V], F32, name=f"yo{g}{t}", tag="yout", bufs=4, align_bytes=64)
+            for n in range(2):
+                cols = slice(HALF * n, HALF * (n + 1))
+                bank = psum.tile([P, HALF], F32, name=f"y{g}{t}{n}", tag="tr", bufs=4)
+                for k in range(2):
+                    w = (wp[:, k, 2 * HALF * n : 2 * HALF * (n + 1)].bitcast(FP4X4), wp_sc[:, k, cols])
+                    mx(bank[:], stationary(ht_q[g, k], t), w, k == 0, k == 1)
+                if engines[n] == "v":
+                    nc.vector.tensor_copy(out=x[:, cols], in_=bank[:])
+                else:
+                    nc.scalar.copy(out=x[:, cols], in_=bank[:])
+                if g == 1:
+                    nc.sync.dma_start(out=y_v[g, t][:, cols], in_=x[:, cols])
+            if g == 0:
+                nc.sync.dma_start(out=y_v[g, t], in_=x[:])
+
+        def pooled(n, j, on_vector):
+            bank = psum.tile([P, HALF], F32, name=f"c{n}{j}", tag="acc", bufs=4)
+            for g in range(2):
+                mx(bank[:], stationary(pl_q[g], j), moving(hc_q[g, n]), g == 0, g == 1)
+            x = ring.tile([P, HALF], F32, name=f"co{n}{j}", tag="cout", bufs=4, align_bytes=64)
+            dst = x[:].rearrange("p (k u e) -> p k u e", u=2, e=2)
+            src = bank[:].rearrange("p (u k e) -> p k u e", u=2, e=2)
+            if on_vector:
+                nc.vector.tensor_copy(out=dst, in_=src)
+            else:
+                nc.scalar.copy(out=dst, in_=src)
+            nc.sync.dma_start(out=c_v[j][:, HALF * n : HALF * (n + 1)], in_=x[:])
+
+        wp = kept("wp", [P, 2, 2 * V], U8)
+        pl_raw = kept("pl_raw", [P, 4, M], U8)
+        pl_scale = kept("pl_scale", [P, M], F32)
+
+        load_act(0, 0, 0)
+        load_act(0, 0, 1)
+        load_w(0, 0)
+        load_act(0, 1, 0)
+        load_w(0, 1)
+        load_act(0, 1, 1)
+        load_w(0, 2)
+        load_act(0, 2, 0)
+        load_w(0, 3)
+        load_act(0, 2, 1)
+        load_w(0, 4)
+        load_w(0, 5)
+        load_res(0, 0)
+        load_act(1, 0, 0)
+        load_w(1, 0)
+        load_act(1, 0, 1)
+        load_w(1, 1)
+        load_act(1, 1, 0)
+        load_w(1, 2)
+        load_act(1, 1, 1)
+        load_w(1, 3)
+        load_act(1, 2, 0)
+        load_w(1, 4)
+        load_act(1, 2, 1)
+        load_w(1, 5)
+        load_res(0, 1)
+        nc.sync.dma_start(out=wp[:], in_=wp_words.rearrange("g p n -> p g n"))
+        for q in range(4):
+            nc.sync.dma_start(
+                out=wp_sc[32 * q : 32 * q + 4].bitcast(I32),
+                in_=wp_scales[:, 4 * q : 4 * q + 4, :].rearrange("g r n -> r g n").bitcast(I32),
+            )
+        load_res(1, 0)
+        nc.sync.dma_start(out=pl_raw[:], in_=pool_bytes.rearrange("(p j) m -> p j m", j=4))
+        nc.sync.dma_start(out=pl_scale[:], in_=pool_scale.rearrange("o m -> (o m)").partition_broadcast(P))
+        load_res(1, 1)
+
+        def turn_pair(g, s, b):
+            turn_act(g, 2 * s, b)
+            turn_act(g, 2 * s + 1, b)
+
+        def sweep(g, n, k):
+            for t in range(4):
+                write_stream(g, n, k, t)
+
+        turn_pair(0, 0, 0)
+        turn_pair(0, 0, 1)
+        group_w(0, 0)
+        quant_act(0, 0)
+        quant_w(0, 0)
+        quant_act(0, 1)
+        turn_pair(0, 1, 0)
+        sweep(0, 0, 0)
+        group_w(0, 1)
+        quant_w(0, 1)
+        turn_pair(0, 1, 1)
+        sweep(0, 0, 1)
+        group_w(0, 2)
+        quant_act(0, 2)
+        quant_w(0, 2)
+        quant_act(0, 3)
+        turn_pair(0, 2, 0)
+        sweep(0, 0, 2)
+        group_w(0, 3)
+        quant_w(0, 3)
+        turn_pair(0, 2, 1)
+        sweep(0, 0, 3)
+        group_w(0, 4)
+        quant_act(0, 4)
+        quant_w(0, 4)
+        group_w(0, 5)
+        quant_act(0, 5)
+        quant_w(0, 5)
+        sweep(0, 0, 4)
+        sweep(0, 0, 5)
+
+        group_w(1, 0)
+        turn_pair(1, 0, 0)
+        add_res(0, 0, 0)
+        add_res(0, 0, 1)
+        quant_w(1, 0)
+        add_res(0, 0, 2)
+        add_res(0, 0, 3)
+        turn_pair(1, 0, 1)
+        sweep(0, 1, 0)
+        group_w(1, 1)
+        quant_act(1, 0)
+        quant_w(1, 1)
+        turn_pair(1, 1, 0)
+        sweep(0, 1, 1)
+        group_w(1, 2)
+        quant_act(1, 1)
+        quant_w(1, 2)
+        turn_pair(1, 1, 1)
+        sweep(0, 1, 2)
+        group_w(1, 3)
+        quant_act(1, 2)
+        quant_w(1, 3)
+        turn_pair(1, 2, 0)
+        sweep(0, 1, 3)
+        group_w(1, 4)
+        quant_act(1, 3)
+        quant_w(1, 4)
+        group_w(1, 5)
+        turn_pair(1, 2, 1)
+        sweep(0, 1, 4)
+        quant_w(1, 5)
+        quant_act(1, 4)
+        quant_act(1, 5)
+        sweep(0, 1, 5)
+        turn_h(0, 0, 0)
+        turn_h(0, 0, 1)
+        for t in range(4):
+            add_res(0, 1, t)
+        quant_ht(0, 0)
+
+        def stream(g, n, t):
+            for k in range(PASSES):
+                write_stream(g, n, k, t)
+
+        stream(1, 0, 0)
+        stream(1, 0, 1)
+        turn_h(0, 1, 0)
+        turn_h(0, 1, 1)
+        add_res(1, 0, 0)
+        quant_ht(0, 1)
+        add_res(1, 0, 1)
+        stream(1, 0, 2)
+        stream(1, 0, 3)
+        scale_pool(0)
+        scale_pool(1)
+        add_res(1, 0, 2)
+        add_res(1, 0, 3)
+        project(0, 0, "ss")
+        project(0, 1, "ss")
+        project(0, 2, "ss")
+        turn_h(1, 0, 0)
+        turn_h(1, 0, 1)
+        scale_pool(2)
+        scale_pool(3)
+        stream(1, 1, 0)
+        group_hc(0, 0)
+        quant_ht(1, 0)
+        quant_hc(0, 0)
+        group_hc(1, 0)
+        for b in range(2):
+            turn_pool(0, b)
+            turn_pool(1, b)
+        add_res(1, 1, 0)
+        quant_hc(1, 0)
+        stream(1, 1, 1)
+        quant_pool(0)
+        quant_pool(1)
+        stream(1, 1, 2)
+        add_res(1, 1, 1)
+        group_hc(0, 1)
+        turn_h(1, 1, 0)
+        pooled(0, 0, False)
+        pooled(0, 1, False)
+        add_res(1, 1, 2)
+        stream(1, 1, 3)
+        quant_hc(0, 1)
+        pooled(0, 2, False)
+        pooled(0, 3, False)
+        add_res(1, 1, 3)
+        turn_h(1, 1, 1)
+        group_hc(1, 1)
+        project(0, 3, "ss")
+        quant_ht(1, 1)
+        quant_hc(1, 1)
+        for t in range(4):
+            project(1, t, "vs")
+        for j in range(4):
+            pooled(1, j, j % 2 == 1)

@@ -75,35 +75,53 @@ def tile_two_writer_residual_s8_kernel(
             res[g, n] = kept(f"res{g}{n}", [P, 4, HALF], BF16)
             nc.sync.dma_start(out=res[g, n][:], in_=resid_v[g][:, :, HALF * n : HALF * (n + 1)])
 
-        def turn_act(g, k, b):
-            bank = psum.tile([P, 4, P], F32, name=f"tr{g}{k}{b}", tag="tr", bufs=4)
+        def copy_words(bank, grp, lo, engine):
+            copy = nc.vector.tensor_copy if engine == "v" else nc.scalar.copy
+            dst = grp[:].rearrange("p r j -> p (r j)").bitcast(F32)
+            copy(
+                out=dst[:, lo : lo + 512].rearrange("p (t r u) -> p t r u", t=2, u=2),
+                in_=bank[:].rearrange("p (t u) r -> p t r u", u=2),
+            )
+
+        def turn_act(g, k, b, engine="s"):
+            bank = psum.tile([P, 4, P], F32, name=f"tr{g}{k}{b}", tag="tr", bufs=2)
             words = act_raw[g, k // 2, b][:].rearrange("p t c -> p (t c)").bitcast(F32)
             for t in range(2):
                 for u in range(2):
                     first = 512 * t + 256 * (k % 2) + u
                     nc.tensor.transpose(bank[:, 2 * t + u, :], words[:, first : first + 255 : 2], ident[:])
-            if (g, k) not in act_grp:
-                act_grp[g, k] = ring.tile([P, 512, 4], BF16, name=f"ag{g}{k}", tag="grp", bufs=6, align_bytes=64)
-            dst = act_grp[g, k][:].rearrange("p r j -> p (r j)").bitcast(F32)
-            nc.scalar.copy(
-                out=dst[:, 512 * b : 512 * (b + 1)].rearrange("p (t r u) -> p t r u", t=2, u=2),
-                in_=bank[:].rearrange("p (t u) r -> p t r u", u=2),
-            )
+            if g == 1:
+                grp = ring.tile([P, 256, 4], BF16, name=f"ah{k}{b}", tag="grph", bufs=4, align_bytes=64)
+                act_grp[g, k, b] = grp
+                lo = 0
+            else:
+                if b == 0:
+                    act_grp[g, k] = ring.tile([P, 512, 4], BF16, name=f"ag{g}{k}", tag="grp", bufs=4, align_bytes=64)
+                grp = act_grp[g, k]
+                lo = 512 * b
+            copy_words(bank, grp, lo, engine)
 
-        def quantize(label, grp):
-            codes = kept(label + "_c", [P, 512], U32)
-            scales = kept(label + "_s", [P, 512], U8)
+        def quantize(label, grp, width=512):
+            codes = kept(label + "_c", [P, width], U32)
+            scales = kept(label + "_s", [P, width], U8)
             nc.vector.quantize_mx(
-                out=codes[:].bitcast(FP8X4), scales=scales[:], in_=grp[:].rearrange("p c j -> p (c j)")
+                out=codes[:].bitcast(FP8X4), scales=scales[:], in_=grp.rearrange("p c j -> p (c j)")
             )
             return codes, scales
 
-        def quant_act(g, k):
-            act_q[g, k] = quantize(f"aq{g}{k}", act_grp[g, k])
+        def quant_act(k):
+            q = quantize(f"aq{k}", act_grp[0, k][:])
+            for t in range(4):
+                act_q[0, k, t] = stationary(q, t)
 
-        def interleave(label, src):
+        def quant_act1(k, b):
+            q = quantize(f"ar{k}{b}", act_grp[1, k, b][:], 256)
+            for t in range(2):
+                act_q[1, k, 2 * b + t] = stationary(q, t)
+
+        def interleave(label, src, v_cols=V_COLS):
             x = ring.tile([P, 512, 4], BF16, name=label, tag="wgrp", bufs=3, align_bytes=64)
-            for copy, lo, hi in ((nc.vector.tensor_copy, 0, V_COLS), (nc.scalar.copy, V_COLS, 512)):
+            for copy, lo, hi in ((nc.vector.tensor_copy, 0, v_cols), (nc.scalar.copy, v_cols, 512)):
                 copy(
                     out=x[:, lo:hi, :].rearrange("p (c i) j -> p c j i", i=4),
                     in_=src[:, :, lo:hi].rearrange("p j (c i) -> p c j i", i=4),
@@ -114,7 +132,7 @@ def tile_two_writer_residual_s8_kernel(
             w_grp[n, k] = interleave(f"wg{n}{k}", w_raw[n, k])
 
         def quant_w(n, k):
-            w_q[n, k] = quantize(f"wq{n}{k}", w_grp[n, k])
+            w_q[n, k] = quantize(f"wq{n}{k}", w_grp[n, k][:])
 
         def mx(out, a, b, start, stop):
             nc.tensor.matmul_mx(
@@ -130,8 +148,8 @@ def tile_two_writer_residual_s8_kernel(
 
         def write_stream(g, n, k, t):
             if k == 0:
-                acc[g, n, t] = psum.tile([P, HALF], F32, name=f"acc{g}{n}{t}", tag="acc", bufs=4)
-            mx(acc[g, n, t][:], stationary(act_q[g, k], t), moving(w_q[n, k]), k == 0, k == PASSES - 1)
+                acc[g, n, t] = psum.tile([P, HALF], F32, name=f"acc{g}{n}{t}", tag="acc", bufs=6)
+            mx(acc[g, n, t][:], act_q[g, k, t], moving(w_q[n, k]), k == 0, k == PASSES - 1)
 
         def add_res(g, n, t):
             if t == 0:
@@ -143,29 +161,33 @@ def tile_two_writer_residual_s8_kernel(
                 op=ADD,
             )
 
-        def turn_h(g, n, b):
-            bank = psum.tile([P, 4, P], F32, name=f"ht{g}{n}{b}", tag="tr", bufs=4)
+        def turn_h(g, n, b, engine="s"):
+            tag, bufs = ("tr", 2) if n == 0 else ("acc", 6)
+            bank = psum.tile([P, 4, P], F32, name=f"ht{g}{n}{b}", tag=tag, bufs=bufs)
             words = h[g, n][:].rearrange("p t c -> p (t c)").bitcast(F32)
             for t in range(2):
                 for u in range(2):
                     first = 256 * (2 * b + t) + P * u
                     nc.tensor.transpose(bank[:, 2 * t + u, :], words[:, first : first + P], ident[:])
             if b == 0:
-                ht_grp[g, n] = ring.tile([P, 512, 4], BF16, name=f"hg{g}{n}", tag="grp", bufs=6, align_bytes=64)
-            dst = ht_grp[g, n][:].rearrange("p r j -> p (r j)").bitcast(F32)
-            nc.scalar.copy(
-                out=dst[:, 512 * b : 512 * (b + 1)].rearrange("p (t r u) -> p t r u", t=2, u=2),
-                in_=bank[:].rearrange("p (t u) r -> p t r u", u=2),
-            )
+                ht_grp[g, n] = ring.tile([P, 512, 4], BF16, name=f"hg{g}{n}", tag="grp", bufs=4, align_bytes=64)
+            copy_words(bank, ht_grp[g, n], 512 * b, engine)
 
         def quant_ht(g, n):
-            ht_q[g, n] = quantize(f"hq{g}{n}", ht_grp[g, n])
+            q = quantize(f"hq{g}{n}", ht_grp[g, n][:])
+            for t in range(4):
+                ht_q[g, n, t] = stationary(q, t)
 
-        def group_hc(g, n):
-            hc_grp[g, n] = interleave(f"hcg{g}{n}", h[g, n])
+        def quant_ht_pair(g, n, b):
+            q = quantize(f"hq{g}{n}{b}", ht_grp[g, n][:, 256 * b : 256 * (b + 1), :], 256)
+            for t in range(2):
+                ht_q[g, n, 2 * b + t] = stationary(q, t)
+
+        def group_hc(g, n, v_cols=V_COLS):
+            hc_grp[g, n] = interleave(f"hcg{g}{n}", h[g, n], v_cols)
 
         def quant_hc(g, n):
-            hc_q[g, n] = quantize(f"hcq{g}{n}", hc_grp[g, n])
+            hc_q[g, n] = quantize(f"hcq{g}{n}", hc_grp[g, n][:])
 
         def scale_pool(j):
             if j % 2 == 0:
@@ -174,46 +196,42 @@ def tile_two_writer_residual_s8_kernel(
                 out=pl_val[j // 2][:, j % 2, :], in0=pl_raw[:, j, :].bitcast(FP8), in1=pl_scale[:], op=MULT
             )
 
-        def turn_pool(k, b):
-            bank = psum.tile([P, 4, P], F32, name=f"pt{k}{b}", tag="tr", bufs=4)
+        def turn_pool(k, b, engine="s"):
+            bank = psum.tile([P, 4, P], F32, name=f"pt{k}{b}", tag="acc", bufs=6)
             words = pl_val[b][:].rearrange("p j c -> p (j c)").bitcast(F32)
             for t in range(2):
                 for u in range(2):
                     first = 512 * t + 256 * k + u
                     nc.tensor.transpose(bank[:, 2 * t + u, :], words[:, first : first + 255 : 2], ident[:])
             if b == 0:
-                pl_grp[k] = ring.tile([P, 512, 4], BF16, name=f"pg{k}", tag="grp", bufs=6, align_bytes=64)
-            dst = pl_grp[k][:].rearrange("p r j -> p (r j)").bitcast(F32)
-            nc.scalar.copy(
-                out=dst[:, 512 * b : 512 * (b + 1)].rearrange("p (t r u) -> p t r u", t=2, u=2),
-                in_=bank[:].rearrange("p (t u) r -> p t r u", u=2),
-            )
+                pl_grp[k] = ring.tile([P, 512, 4], BF16, name=f"pg{k}", tag="grp", bufs=4, align_bytes=64)
+            copy_words(bank, pl_grp[k], 512 * b, engine)
 
         def quant_pool(k):
-            pl_q[k] = quantize(f"pq{k}", pl_grp[k])
+            pl_q[k] = quantize(f"pq{k}", pl_grp[k][:])
 
         def project(g, t, engines):
-            x = ring.tile([P, V], F32, name=f"yo{g}{t}", tag="yout", bufs=4, align_bytes=64)
+            x = ring.tile([P, V], F32, name=f"yo{g}{t}", tag="out", bufs=6, align_bytes=64)
             for n in range(2):
                 cols = slice(HALF * n, HALF * (n + 1))
-                bank = psum.tile([P, HALF], F32, name=f"y{g}{t}{n}", tag="tr", bufs=4)
+                bank = psum.tile([P, HALF], F32, name=f"y{g}{t}{n}", tag="acc", bufs=6)
                 for k in range(2):
                     w = (wp[:, k, 2 * HALF * n : 2 * HALF * (n + 1)].bitcast(FP4X4), wp_sc[:, k, cols])
-                    mx(bank[:], stationary(ht_q[g, k], t), w, k == 0, k == 1)
+                    mx(bank[:], ht_q[g, k, t], w, k == 0, k == 1)
                 if engines[n] == "v":
                     nc.vector.tensor_copy(out=x[:, cols], in_=bank[:])
                 else:
                     nc.scalar.copy(out=x[:, cols], in_=bank[:])
-                if g == 1:
+                if g == 1 and t == 3:
                     nc.sync.dma_start(out=y_v[g, t][:, cols], in_=x[:, cols])
-            if g == 0:
+            if not (g == 1 and t == 3):
                 nc.sync.dma_start(out=y_v[g, t], in_=x[:])
 
         def pooled(n, j, on_vector):
-            bank = psum.tile([P, HALF], F32, name=f"c{n}{j}", tag="acc", bufs=4)
+            bank = psum.tile([P, HALF], F32, name=f"c{n}{j}", tag="acc", bufs=6)
             for g in range(2):
                 mx(bank[:], stationary(pl_q[g], j), moving(hc_q[g, n]), g == 0, g == 1)
-            x = ring.tile([P, HALF], F32, name=f"co{n}{j}", tag="cout", bufs=4, align_bytes=64)
+            x = ring.tile([P, HALF], F32, name=f"co{n}{j}", tag="out", bufs=6, align_bytes=64)
             dst = x[:].rearrange("p (k u e) -> p k u e", u=2, e=2)
             src = bank[:].rearrange("p (u k e) -> p k u e", u=2, e=2)
             if on_vector:
@@ -226,177 +244,182 @@ def tile_two_writer_residual_s8_kernel(
         pl_raw = kept("pl_raw", [P, 4, M], U8)
         pl_scale = kept("pl_scale", [P, M], F32)
 
-        load_act(0, 0, 0)
-        load_act(0, 0, 1)
-        load_w(0, 0)
-        load_act(0, 1, 0)
-        load_w(0, 1)
-        load_act(0, 1, 1)
-        load_w(0, 2)
-        load_act(0, 2, 0)
-        load_w(0, 3)
-        load_act(0, 2, 1)
-        load_w(0, 4)
-        load_w(0, 5)
-        load_res(0, 0)
-        load_act(1, 0, 0)
-        load_w(1, 0)
+        for s in range(3):
+            load_act(0, s, 0)
+            load_act(0, s, 1)
+            load_w(0, 2 * s)
+            load_act(1, s, 0)
+            load_w(0, 2 * s + 1)
         load_act(1, 0, 1)
-        load_w(1, 1)
-        load_act(1, 1, 0)
-        load_w(1, 2)
+        load_res(0, 0)
         load_act(1, 1, 1)
-        load_w(1, 3)
-        load_act(1, 2, 0)
-        load_w(1, 4)
+        load_res(1, 0)
         load_act(1, 2, 1)
-        load_w(1, 5)
+        for k in range(PASSES):
+            load_w(1, k)
         load_res(0, 1)
+        load_res(1, 1)
         nc.sync.dma_start(out=wp[:], in_=wp_words.rearrange("g p n -> p g n"))
         for q in range(4):
             nc.sync.dma_start(
                 out=wp_sc[32 * q : 32 * q + 4].bitcast(I32),
                 in_=wp_scales[:, 4 * q : 4 * q + 4, :].rearrange("g r n -> r g n").bitcast(I32),
             )
-        load_res(1, 0)
         nc.sync.dma_start(out=pl_raw[:], in_=pool_bytes.rearrange("(p j) m -> p j m", j=4))
         nc.sync.dma_start(out=pl_scale[:], in_=pool_scale.rearrange("o m -> (o m)").partition_broadcast(P))
-        load_res(1, 1)
 
-        def turn_pair(g, s, b):
-            turn_act(g, 2 * s, b)
-            turn_act(g, 2 * s + 1, b)
+        def turn_pair(g, s, b, engines="ss"):
+            turn_act(g, 2 * s, b, engines[0])
+            turn_act(g, 2 * s + 1, b, engines[1])
 
-        def sweep(g, n, k):
-            for t in range(4):
+        def quant_pair1(s, b):
+            quant_act1(2 * s, b)
+            quant_act1(2 * s + 1, b)
+
+        def sweep(g, n, k, tiles):
+            for t in tiles:
                 write_stream(g, n, k, t)
+
+        ALL, LOW, HIGH = range(4), range(2), range(2, 4)
 
         turn_pair(0, 0, 0)
         turn_pair(0, 0, 1)
+        quant_act(0)
         group_w(0, 0)
-        quant_act(0, 0)
+        quant_act(1)
         quant_w(0, 0)
-        quant_act(0, 1)
-        turn_pair(0, 1, 0)
-        sweep(0, 0, 0)
-        group_w(0, 1)
-        quant_w(0, 1)
-        turn_pair(0, 1, 1)
-        sweep(0, 0, 1)
-        group_w(0, 2)
-        quant_act(0, 2)
-        quant_w(0, 2)
-        quant_act(0, 3)
-        turn_pair(0, 2, 0)
-        sweep(0, 0, 2)
-        group_w(0, 3)
-        quant_w(0, 3)
-        turn_pair(0, 2, 1)
-        sweep(0, 0, 3)
-        group_w(0, 4)
-        quant_act(0, 4)
-        quant_w(0, 4)
-        group_w(0, 5)
-        quant_act(0, 5)
-        quant_w(0, 5)
-        sweep(0, 0, 4)
-        sweep(0, 0, 5)
-
-        group_w(1, 0)
         turn_pair(1, 0, 0)
-        add_res(0, 0, 0)
-        add_res(0, 0, 1)
-        quant_w(1, 0)
-        add_res(0, 0, 2)
-        add_res(0, 0, 3)
-        turn_pair(1, 0, 1)
-        sweep(0, 1, 0)
-        group_w(1, 1)
-        quant_act(1, 0)
-        quant_w(1, 1)
+        quant_act1(0, 0)
+        group_w(0, 1)
+        quant_act1(1, 0)
+        sweep(0, 0, 0, ALL)
+        sweep(1, 0, 0, LOW)
+        quant_w(0, 1)
+        turn_pair(0, 1, 0)
+        turn_pair(0, 1, 1)
+        sweep(0, 0, 1, ALL)
+        sweep(1, 0, 1, LOW)
+        group_w(0, 2)
+        quant_act(2)
+        quant_act(3)
+        quant_w(0, 2)
+        group_w(0, 3)
         turn_pair(1, 1, 0)
-        sweep(0, 1, 1)
-        group_w(1, 2)
-        quant_act(1, 1)
-        quant_w(1, 2)
-        turn_pair(1, 1, 1)
-        sweep(0, 1, 2)
-        group_w(1, 3)
-        quant_act(1, 2)
-        quant_w(1, 3)
+        quant_w(0, 3)
+        quant_pair1(1, 0)
+        for k in range(2, 4):
+            sweep(0, 0, k, ALL)
+        for k in range(2, 4):
+            sweep(1, 0, k, LOW)
+        group_w(0, 4)
+        turn_pair(0, 2, 0)
+        quant_w(0, 4)
+        turn_pair(0, 2, 1)
         turn_pair(1, 2, 0)
-        sweep(0, 1, 3)
-        group_w(1, 4)
-        quant_act(1, 3)
-        quant_w(1, 4)
-        group_w(1, 5)
+        group_w(0, 5)
+        quant_act(4)
+        quant_act(5)
+        quant_pair1(2, 0)
+        quant_w(0, 5)
+        turn_pair(1, 0, 1)
+        quant_pair1(0, 1)
+        for k in range(4, 6):
+            sweep(0, 0, k, ALL)
+            sweep(1, 0, k, LOW)
+
+        for t in ALL:
+            add_res(0, 0, t)
+        for t in LOW:
+            add_res(1, 0, t)
+        for k in range(2):
+            sweep(1, 0, k, HIGH)
+        turn_pair(1, 1, 1)
+        group_w(1, 0)
+        quant_pair1(1, 1)
         turn_pair(1, 2, 1)
-        sweep(0, 1, 4)
-        quant_w(1, 5)
-        quant_act(1, 4)
-        quant_act(1, 5)
-        sweep(0, 1, 5)
+        group_w(1, 1)
+        quant_pair1(2, 1)
         turn_h(0, 0, 0)
         turn_h(0, 0, 1)
-        for t in range(4):
-            add_res(0, 1, t)
-        quant_ht(0, 0)
+        group_w(1, 2)
+        quant_w(1, 0)
+        quant_w(1, 1)
+        for k in range(2, 6):
+            sweep(1, 0, k, HIGH)
+        for t in HIGH:
+            add_res(1, 0, t)
+        quant_w(1, 2)
 
         def stream(g, n, t):
             for k in range(PASSES):
                 write_stream(g, n, k, t)
 
-        stream(1, 0, 0)
-        stream(1, 0, 1)
-        turn_h(0, 1, 0)
-        turn_h(0, 1, 1)
-        add_res(1, 0, 0)
-        quant_ht(0, 1)
-        add_res(1, 0, 1)
-        stream(1, 0, 2)
-        stream(1, 0, 3)
-        scale_pool(0)
-        scale_pool(1)
-        add_res(1, 0, 2)
-        add_res(1, 0, 3)
-        project(0, 0, "ss")
-        project(0, 1, "ss")
-        project(0, 2, "ss")
+        sweep(0, 1, 0, ALL)
+        group_w(1, 3)
+        sweep(0, 1, 1, ALL)
+        group_w(1, 4)
+        sweep(1, 1, 0, LOW)
+        quant_w(1, 3)
+        sweep(0, 1, 2, ALL)
+        sweep(1, 1, 1, LOW)
+        quant_w(1, 4)
+        group_w(1, 5)
+        sweep(0, 1, 3, ALL)
+        sweep(1, 1, 2, LOW)
+        quant_ht(0, 0)
+        quant_w(1, 5)
+        sweep(0, 1, 4, ALL)
+        sweep(1, 1, 3, LOW)
+        group_hc(0, 0, 128)
+        group_hc(1, 0, 128)
+        quant_hc(0, 0)
+        quant_hc(1, 0)
+        sweep(0, 1, 5, ALL)
         turn_h(1, 0, 0)
         turn_h(1, 0, 1)
+        for t in ALL:
+            add_res(0, 1, t)
+        quant_ht(1, 0)
+        sweep(1, 1, 4, LOW)
+        sweep(1, 1, 5, LOW)
+        for t in LOW:
+            add_res(1, 1, t)
+        turn_h(0, 1, 0)
+        turn_h(0, 1, 1)
+        scale_pool(0)
+        quant_ht(0, 1)
+        stream(1, 1, 2)
+        turn_h(1, 1, 0)
+        scale_pool(1)
+        project(0, 0, "ss")
+        add_res(1, 1, 2)
+        quant_ht_pair(1, 1, 0)
+        project(0, 1, "ss")
         scale_pool(2)
         scale_pool(3)
-        stream(1, 1, 0)
-        group_hc(0, 0)
-        quant_ht(1, 0)
-        quant_hc(0, 0)
-        group_hc(1, 0)
-        for b in range(2):
-            turn_pool(0, b)
-            turn_pool(1, b)
-        add_res(1, 1, 0)
-        quant_hc(1, 0)
-        stream(1, 1, 1)
+        project(0, 2, "ss")
+        project(0, 3, "sv")
+        project(1, 0, "sv")
+        project(1, 1, "sv")
+        turn_pool(0, 0, "s")
+        turn_pool(1, 0, "v")
+        turn_pool(0, 1, "s")
+        turn_pool(1, 1, "v")
         quant_pool(0)
         quant_pool(1)
-        stream(1, 1, 2)
-        add_res(1, 1, 1)
-        group_hc(0, 1)
-        turn_h(1, 1, 0)
-        pooled(0, 0, False)
-        pooled(0, 1, False)
-        add_res(1, 1, 2)
         stream(1, 1, 3)
-        quant_hc(0, 1)
-        pooled(0, 2, False)
-        pooled(0, 3, False)
+        group_hc(0, 1)
         add_res(1, 1, 3)
-        turn_h(1, 1, 1)
+        pooled(0, 0, False)
+        turn_h(1, 1, 1, "s")
+        quant_hc(0, 1)
+        quant_ht_pair(1, 1, 1)
+        pooled(0, 1, False)
         group_hc(1, 1)
-        project(0, 3, "ss")
-        quant_ht(1, 1)
+        pooled(0, 2, True)
+        pooled(0, 3, False)
         quant_hc(1, 1)
-        for t in range(4):
+        for t in range(2, 4):
             project(1, t, "vs")
         for j in range(4):
             pooled(1, j, j % 2 == 1)

@@ -38,6 +38,8 @@ def tile_two_writer_residual_s8_kernel(
 
         ident = kept("ident", [P, P], F32)
         wp_sc = kept("wp_sc", [P, 2, V], U8)
+        zeros = kept("zeros", [P, 512], BF16)
+        nc.vector.memset(zeros[:], 0.0)
         make_identity(nc, ident[:])
         nc.gpsimd.memset(wp_sc[:].rearrange("p g n -> p (g n)").bitcast(I32), 0)
 
@@ -83,8 +85,12 @@ def tile_two_writer_residual_s8_kernel(
                 in_=bank[:].rearrange("p (t u) r -> p t r u", u=2),
             )
 
+        def warm(i):
+            bank = psum.tile([P, HALF], F32, name=f"warm{i}", tag="bank", bufs=8)
+            nc.tensor.matmul(bank[:], lhsT=zeros[:, :P], rhs=zeros[:], start=True, stop=True)
+
         def turn_act(g, k, b, engine="s"):
-            bank = psum.tile([P, 4, P], F32, name=f"tr{g}{k}{b}", tag="tr", bufs=2)
+            bank = psum.tile([P, 4, P], F32, name=f"tr{g}{k}{b}", tag="bank", bufs=8)
             words = act_raw[g, k // 2, b][:].rearrange("p t c -> p (t c)").bitcast(F32)
             for t in range(2):
                 for u in range(2):
@@ -95,7 +101,7 @@ def tile_two_writer_residual_s8_kernel(
                 act_grp[g, k, b] = grp
                 lo = 0
             else:
-                if b == 0:
+                if (g, k) not in act_grp:
                     act_grp[g, k] = ring.tile([P, 512, 4], BF16, name=f"ag{g}{k}", tag="grp", bufs=4, align_bytes=64)
                 grp = act_grp[g, k]
                 lo = 512 * b
@@ -122,14 +128,15 @@ def tile_two_writer_residual_s8_kernel(
         def interleave(label, src, v_cols=V_COLS):
             x = ring.tile([P, 512, 4], BF16, name=label, tag="wgrp", bufs=3, align_bytes=64)
             for copy, lo, hi in ((nc.vector.tensor_copy, 0, v_cols), (nc.scalar.copy, v_cols, 512)):
-                copy(
-                    out=x[:, lo:hi, :].rearrange("p (c i) j -> p c j i", i=4),
-                    in_=src[:, :, lo:hi].rearrange("p j (c i) -> p c j i", i=4),
-                )
+                if lo < hi:
+                    copy(
+                        out=x[:, lo:hi, :].rearrange("p (c i) j -> p c j i", i=4),
+                        in_=src[:, :, lo:hi].rearrange("p j (c i) -> p c j i", i=4),
+                    )
             return x
 
-        def group_w(n, k):
-            w_grp[n, k] = interleave(f"wg{n}{k}", w_raw[n, k])
+        def group_w(n, k, v_cols):
+            w_grp[n, k] = interleave(f"wg{n}{k}", w_raw[n, k], v_cols)
 
         def quant_w(n, k):
             w_q[n, k] = quantize(f"wq{n}{k}", w_grp[n, k][:])
@@ -148,11 +155,11 @@ def tile_two_writer_residual_s8_kernel(
 
         def write_stream(g, n, k, t):
             if k == 0:
-                acc[g, n, t] = psum.tile([P, HALF], F32, name=f"acc{g}{n}{t}", tag="acc", bufs=6)
+                acc[g, n, t] = psum.tile([P, HALF], F32, name=f"acc{g}{n}{t}", tag="bank", bufs=8)
             mx(acc[g, n, t][:], act_q[g, k, t], moving(w_q[n, k]), k == 0, k == PASSES - 1)
 
         def add_res(g, n, t):
-            if t == 0:
+            if (g, n) not in h:
                 h[g, n] = ring.tile([P, 4, HALF], BF16, name=f"h{g}{n}", tag="h", bufs=4, align_bytes=64)
             nc.vector.tensor_tensor(
                 out=h[g, n][:, t, :].rearrange("p (u k e) -> p u k e", u=2, e=2),
@@ -162,8 +169,7 @@ def tile_two_writer_residual_s8_kernel(
             )
 
         def turn_h(g, n, b, engine="s"):
-            tag, bufs = ("tr", 2) if n == 0 else ("acc", 6)
-            bank = psum.tile([P, 4, P], F32, name=f"ht{g}{n}{b}", tag=tag, bufs=bufs)
+            bank = psum.tile([P, 4, P], F32, name=f"ht{g}{n}{b}", tag="bank", bufs=8)
             words = h[g, n][:].rearrange("p t c -> p (t c)").bitcast(F32)
             for t in range(2):
                 for u in range(2):
@@ -197,13 +203,13 @@ def tile_two_writer_residual_s8_kernel(
             )
 
         def turn_pool(k, b, engine="s"):
-            bank = psum.tile([P, 4, P], F32, name=f"pt{k}{b}", tag="acc", bufs=6)
+            bank = psum.tile([P, 4, P], F32, name=f"pt{k}{b}", tag="bank", bufs=8)
             words = pl_val[b][:].rearrange("p j c -> p (j c)").bitcast(F32)
             for t in range(2):
                 for u in range(2):
                     first = 512 * t + 256 * k + u
                     nc.tensor.transpose(bank[:, 2 * t + u, :], words[:, first : first + 255 : 2], ident[:])
-            if b == 0:
+            if k not in pl_grp:
                 pl_grp[k] = ring.tile([P, 512, 4], BF16, name=f"pg{k}", tag="grp", bufs=4, align_bytes=64)
             copy_words(bank, pl_grp[k], 512 * b, engine)
 
@@ -214,7 +220,7 @@ def tile_two_writer_residual_s8_kernel(
             x = ring.tile([P, V], F32, name=f"yo{g}{t}", tag="out", bufs=6, align_bytes=64)
             for n in range(2):
                 cols = slice(HALF * n, HALF * (n + 1))
-                bank = psum.tile([P, HALF], F32, name=f"y{g}{t}{n}", tag="acc", bufs=6)
+                bank = psum.tile([P, HALF], F32, name=f"y{g}{t}{n}", tag="bank", bufs=8)
                 for k in range(2):
                     w = (wp[:, k, 2 * HALF * n : 2 * HALF * (n + 1)].bitcast(FP4X4), wp_sc[:, k, cols])
                     mx(bank[:], ht_q[g, k, t], w, k == 0, k == 1)
@@ -227,14 +233,14 @@ def tile_two_writer_residual_s8_kernel(
             if not (g == 1 and t == 3):
                 nc.sync.dma_start(out=y_v[g, t], in_=x[:])
 
-        def pooled(n, j, on_vector):
-            bank = psum.tile([P, HALF], F32, name=f"c{n}{j}", tag="acc", bufs=6)
+        def pooled(n, j, engine):
+            bank = psum.tile([P, HALF], F32, name=f"c{n}{j}", tag="bank", bufs=8)
             for g in range(2):
                 mx(bank[:], stationary(pl_q[g], j), moving(hc_q[g, n]), g == 0, g == 1)
             x = ring.tile([P, HALF], F32, name=f"co{n}{j}", tag="out", bufs=6, align_bytes=64)
             dst = x[:].rearrange("p (k u e) -> p k u e", u=2, e=2)
             src = bank[:].rearrange("p (u k e) -> p k u e", u=2, e=2)
-            if on_vector:
+            if engine == "v":
                 nc.vector.tensor_copy(out=dst, in_=src)
             else:
                 nc.scalar.copy(out=dst, in_=src)
@@ -244,31 +250,23 @@ def tile_two_writer_residual_s8_kernel(
         pl_raw = kept("pl_raw", [P, 4, M], U8)
         pl_scale = kept("pl_scale", [P, M], F32)
 
-        for s in range(3):
-            load_act(0, s, 0)
-            load_act(0, s, 1)
-            load_w(0, 2 * s)
-            load_act(1, s, 0)
-            load_w(0, 2 * s + 1)
-        load_act(1, 0, 1)
-        load_res(0, 0)
-        load_act(1, 1, 1)
-        load_res(1, 0)
-        load_act(1, 2, 1)
-        for k in range(PASSES):
-            load_w(1, k)
-        load_res(0, 1)
-        load_res(1, 1)
-        nc.sync.dma_start(out=wp[:], in_=wp_words.rearrange("g p n -> p g n"))
-        for q in range(4):
-            nc.sync.dma_start(
-                out=wp_sc[32 * q : 32 * q + 4].bitcast(I32),
-                in_=wp_scales[:, 4 * q : 4 * q + 4, :].rearrange("g r n -> r g n").bitcast(I32),
-            )
-        nc.sync.dma_start(out=pl_raw[:], in_=pool_bytes.rearrange("(p j) m -> p j m", j=4))
-        nc.sync.dma_start(out=pl_scale[:], in_=pool_scale.rearrange("o m -> (o m)").partition_broadcast(P))
+        def load_wp():
+            nc.sync.dma_start(out=wp[:], in_=wp_words.rearrange("g p n -> p g n"))
 
-        def turn_pair(g, s, b, engines="ss"):
+        def load_wp_sc():
+            for q in range(4):
+                nc.sync.dma_start(
+                    out=wp_sc[32 * q : 32 * q + 4].bitcast(I32),
+                    in_=wp_scales[:, 4 * q : 4 * q + 4, :].rearrange("g r n -> r g n").bitcast(I32),
+                )
+
+        def load_pool():
+            nc.sync.dma_start(out=pl_raw[:], in_=pool_bytes.rearrange("(p j) m -> p j m", j=4))
+
+        def load_pool_scale():
+            nc.sync.dma_start(out=pl_scale[:], in_=pool_scale.rearrange("o m -> (o m)").partition_broadcast(P))
+
+        def turn_pair(g, s, b, engines):
             turn_act(g, 2 * s, b, engines[0])
             turn_act(g, 2 * s + 1, b, engines[1])
 
@@ -280,146 +278,191 @@ def tile_two_writer_residual_s8_kernel(
             for t in tiles:
                 write_stream(g, n, k, t)
 
+        def add_pair(g, n, b):
+            add_res(g, n, 2 * b)
+            add_res(g, n, 2 * b + 1)
+
         ALL, LOW, HIGH = range(4), range(2), range(2, 4)
 
-        turn_pair(0, 0, 0)
-        turn_pair(0, 0, 1)
-        quant_act(0)
-        group_w(0, 0)
-        quant_act(1)
-        quant_w(0, 0)
-        turn_pair(1, 0, 0)
-        quant_act1(0, 0)
-        group_w(0, 1)
-        quant_act1(1, 0)
-        sweep(0, 0, 0, ALL)
-        sweep(1, 0, 0, LOW)
-        quant_w(0, 1)
-        turn_pair(0, 1, 0)
-        turn_pair(0, 1, 1)
-        sweep(0, 0, 1, ALL)
-        sweep(1, 0, 1, LOW)
-        group_w(0, 2)
-        quant_act(2)
-        quant_act(3)
-        quant_w(0, 2)
-        group_w(0, 3)
-        turn_pair(1, 1, 0)
-        quant_w(0, 3)
-        quant_pair1(1, 0)
-        for k in range(2, 4):
-            sweep(0, 0, k, ALL)
-        for k in range(2, 4):
-            sweep(1, 0, k, LOW)
-        group_w(0, 4)
-        turn_pair(0, 2, 0)
-        quant_w(0, 4)
-        turn_pair(0, 2, 1)
-        turn_pair(1, 2, 0)
-        group_w(0, 5)
-        quant_act(4)
-        quant_act(5)
-        quant_pair1(2, 0)
-        quant_w(0, 5)
-        turn_pair(1, 0, 1)
+        load_act(0, 0, 1)
+        warm(14)
+        warm(8)
+        load_act(0, 0, 0)
+        warm(17)
+        warm(18)
+        load_act(1, 0, 1)
+        turn_pair(0, 0, 1, "sv")
+        turn_pair(0, 0, 0, "sv")
+        load_act(0, 2, 0)
+        load_w(0, 0)
+        load_w(0, 1)
+        turn_pair(1, 0, 1, "vs")
+        load_act(1, 0, 0)
         quant_pair1(0, 1)
-        for k in range(4, 6):
-            sweep(0, 0, k, ALL)
-            sweep(1, 0, k, LOW)
-
-        for t in ALL:
-            add_res(0, 0, t)
-        for t in LOW:
-            add_res(1, 0, t)
-        for k in range(2):
-            sweep(1, 0, k, HIGH)
-        turn_pair(1, 1, 1)
-        group_w(1, 0)
-        quant_pair1(1, 1)
-        turn_pair(1, 2, 1)
-        group_w(1, 1)
+        load_act(0, 2, 1)
+        load_act(1, 1, 0)
+        warm(19)
+        warm(6)
+        group_w(0, 0, 192)
+        group_w(0, 1, 384)
+        turn_pair(0, 2, 0, "ss")
+        quant_act(0)
+        warm(1)
+        load_act(1, 2, 1)
+        load_act(1, 1, 1)
+        quant_w(0, 0)
+        warm(20)
+        turn_pair(1, 0, 0, "sv")
+        quant_w(0, 1)
+        quant_pair1(0, 0)
+        load_w(0, 3)
+        turn_pair(0, 2, 1, "ss")
+        sweep(1, 0, 0, HIGH)
+        load_act(1, 2, 0)
+        load_act(0, 1, 1)
+        load_act(0, 1, 0)
+        quant_act(1)
+        turn_pair(1, 1, 0, "sv")
+        warm(22)
+        load_w(0, 2)
+        load_w(1, 0)
+        warm(11)
+        turn_pair(1, 2, 1, "vs")
+        quant_pair1(1, 0)
+        sweep(1, 0, 0, LOW)
         quant_pair1(2, 1)
-        turn_h(0, 0, 0)
-        turn_h(0, 0, 1)
-        group_w(1, 2)
+        turn_pair(1, 1, 1, "vs")
+        turn_pair(1, 2, 0, "ss")
+        sweep(1, 0, 1, LOW)
+        group_w(0, 3, 512)
+        sweep(1, 0, 1, HIGH)
+        quant_act(4)
+        quant_w(0, 3)
+        quant_pair1(1, 1)
+        turn_pair(0, 1, 1, "ss")
+        load_w(0, 4)
+        group_w(0, 2, 384)
+        turn_pair(0, 1, 0, "sv")
+        load_w(0, 5)
+        quant_w(0, 2)
+        group_w(1, 0, 128)
+        quant_act(2)
+        quant_pair1(2, 0)
+        quant_act(3)
         quant_w(1, 0)
+        sweep(0, 0, 0, ALL)
+        load_w(1, 2)
+        load_w(1, 1)
+        group_w(0, 4, 192)
+        sweep(0, 0, 1, ALL)
+        load_w(1, 3)
+        sweep(1, 0, 2, HIGH)
+        sweep(0, 0, 2, ALL)
+        sweep(1, 0, 3, HIGH)
+        sweep(1, 0, 2, LOW)
+        group_w(0, 5, 128)
+        quant_w(0, 4)
+        quant_act(5)
+        load_res(0, 0)
+        sweep(0, 0, 3, ALL)
+        sweep(1, 0, 3, LOW)
+        quant_w(0, 5)
+        sweep(0, 0, 4, ALL)
+        load_w(1, 4)
+        sweep(0, 0, 5, ALL)
+        group_w(1, 1, 512)
+        sweep(1, 0, 4, LOW)
+        sweep(1, 0, 5, LOW)
+        sweep(1, 0, 4, HIGH)
+        load_pool()
+        sweep(1, 0, 5, HIGH)
         quant_w(1, 1)
-        for k in range(2, 6):
-            sweep(1, 0, k, HIGH)
-        for t in HIGH:
-            add_res(1, 0, t)
-        quant_w(1, 2)
-
-        def stream(g, n, t):
-            for k in range(PASSES):
-                write_stream(g, n, k, t)
-
         sweep(0, 1, 0, ALL)
-        group_w(1, 3)
         sweep(0, 1, 1, ALL)
-        group_w(1, 4)
+        group_w(1, 2, 128)
+        add_pair(0, 0, 0)
+        add_pair(0, 0, 1)
+        load_res(1, 0)
+        load_w(1, 5)
+        load_pool_scale()
+        quant_w(1, 2)
+        group_w(1, 3, 192)
+        group_w(1, 4, 0)
+        load_res(1, 1)
+        add_pair(1, 0, 1)
+        sweep(0, 1, 2, ALL)
+        group_w(1, 5, 0)
         sweep(1, 1, 0, LOW)
         quant_w(1, 3)
-        sweep(0, 1, 2, ALL)
+        add_pair(1, 0, 0)
+        load_wp()
         sweep(1, 1, 1, LOW)
         quant_w(1, 4)
-        group_w(1, 5)
-        sweep(0, 1, 3, ALL)
-        sweep(1, 1, 2, LOW)
-        quant_ht(0, 0)
+        group_hc(0, 0, 0)
         quant_w(1, 5)
-        sweep(0, 1, 4, ALL)
-        sweep(1, 1, 3, LOW)
-        group_hc(0, 0, 128)
-        group_hc(1, 0, 128)
-        quant_hc(0, 0)
-        quant_hc(1, 0)
-        sweep(0, 1, 5, ALL)
-        turn_h(1, 0, 0)
-        turn_h(1, 0, 1)
-        for t in ALL:
-            add_res(0, 1, t)
-        quant_ht(1, 0)
-        sweep(1, 1, 4, LOW)
-        sweep(1, 1, 5, LOW)
-        for t in LOW:
-            add_res(1, 1, t)
-        turn_h(0, 1, 0)
-        turn_h(0, 1, 1)
-        scale_pool(0)
-        quant_ht(0, 1)
-        stream(1, 1, 2)
-        turn_h(1, 1, 0)
-        scale_pool(1)
-        project(0, 0, "ss")
-        add_res(1, 1, 2)
-        quant_ht_pair(1, 1, 0)
-        project(0, 1, "ss")
         scale_pool(2)
         scale_pool(3)
-        project(0, 2, "ss")
-        project(0, 3, "sv")
-        project(1, 0, "sv")
-        project(1, 1, "sv")
+        sweep(0, 1, 3, ALL)
+        sweep(1, 1, 2, LOW)
+        load_res(0, 1)
+        sweep(0, 1, 4, ALL)
+        sweep(1, 1, 3, LOW)
+        group_hc(1, 0, 192)
+        sweep(0, 1, 5, ALL)
+        add_pair(0, 1, 0)
+        add_pair(0, 1, 1)
+        turn_pool(0, 1, "v")
+        turn_pool(1, 1, "s")
+        sweep(1, 1, 4, LOW)
+        sweep(1, 1, 0, HIGH)
+        turn_h(0, 1, 0, "s")
+        turn_h(0, 1, 1, "s")
+        scale_pool(0)
+        scale_pool(1)
+        turn_h(0, 0, 0, "s")
+        turn_h(0, 0, 1, "s")
+        sweep(1, 1, 5, LOW)
+        add_pair(1, 1, 0)
+        sweep(1, 1, 1, HIGH)
+        turn_h(1, 0, 0, "s")
+        turn_h(1, 0, 1, "s")
+        group_hc(0, 1, 256)
+        quant_ht(0, 0)
+        quant_ht(0, 1)
         turn_pool(0, 0, "s")
-        turn_pool(1, 0, "v")
-        turn_pool(0, 1, "s")
-        turn_pool(1, 1, "v")
+        turn_pool(1, 0, "s")
+        quant_hc(1, 0)
         quant_pool(0)
-        quant_pool(1)
-        stream(1, 1, 3)
-        group_hc(0, 1)
-        add_res(1, 1, 3)
-        pooled(0, 0, False)
-        turn_h(1, 1, 1, "s")
+        turn_h(1, 1, 0, "s")
+        quant_hc(0, 0)
         quant_hc(0, 1)
-        quant_ht_pair(1, 1, 1)
-        pooled(0, 1, False)
-        group_hc(1, 1)
-        pooled(0, 2, True)
-        pooled(0, 3, False)
+        sweep(1, 1, 2, HIGH)
+        sweep(1, 1, 3, HIGH)
+        load_wp_sc()
+        quant_ht(1, 0)
+        quant_ht_pair(1, 1, 0)
+        project(0, 0, "ss")
+        sweep(1, 1, 4, HIGH)
+        quant_pool(1)
+        project(0, 2, "ss")
+        project(0, 3, "vs")
+        sweep(1, 1, 5, HIGH)
+        pooled(0, 3, "s")
+        add_pair(1, 1, 1)
+        pooled(0, 2, "v")
+        group_hc(1, 1, 512)
+        project(1, 0, "ss")
+        project(0, 1, "sv")
+        project(1, 1, "sv")
+        turn_h(1, 1, 1, "s")
         quant_hc(1, 1)
-        for t in range(2, 4):
-            project(1, t, "vs")
-        for j in range(4):
-            pooled(1, j, j % 2 == 1)
+        quant_ht_pair(1, 1, 1)
+        pooled(0, 1, "s")
+        pooled(0, 0, "v")
+        pooled(1, 3, "s")
+        project(1, 3, "vs")
+        pooled(1, 2, "s")
+        project(1, 2, "sv")
+        warm(3)
+        pooled(1, 0, "s")
+        pooled(1, 1, "s")

@@ -59,7 +59,7 @@ def tile_two_writer_residual_s8_kernel(
         pl_val, pl_grp, pl_q = {}, {}, {}
 
         def load_act(g, s, b):
-            x = ring.tile([P, 2, 1024], BF16, name=f"act{g}{s}{b}", tag="act", bufs=6, align_bytes=64)
+            x = ring.tile([P, 2, 1024], BF16, name=f"act{g}{s}{b}", tag="raw", bufs=10, align_bytes=64)
             two = slice(2 * b, 2 * b + 2)
             if s == 0:
                 nc.sync.dma_start(out=x[:], in_=attn_v[g][:, two, :])
@@ -68,7 +68,7 @@ def tile_two_writer_residual_s8_kernel(
             act_raw[g, s, b] = x
 
         def load_w(n, k):
-            x = ring.tile([P, 4, HALF], BF16, name=f"w{n}{k}", tag="wraw", bufs=5, align_bytes=64)
+            x = ring.tile([P, 4, HALF], BF16, name=f"w{n}{k}", tag="raw", bufs=10, align_bytes=64)
             rows = wo_v[k] if k < KA else wd_v[k - KA]
             nc.sync.dma_start(out=x[:], in_=rows[:, :, HALF * n : HALF * (n + 1)])
             w_raw[n, k] = x
@@ -76,6 +76,36 @@ def tile_two_writer_residual_s8_kernel(
         def load_res(g, n):
             res[g, n] = kept(f"res{g}{n}", [P, 4, HALF], BF16)
             nc.sync.dma_start(out=res[g, n][:], in_=resid_v[g][:, :, HALF * n : HALF * (n + 1)])
+
+        turned = set()
+
+        def halve(src, label, engine):
+            x = ring.tile([P, 2, 1024], BF16, name=label, tag="halves", bufs=2, align_bytes=64)
+            copy = nc.vector.tensor_copy if engine == "v" else nc.scalar.copy
+            copy(
+                out=x[:].rearrange("p t c -> p (t c)").bitcast(F32).rearrange("p (x u i) -> p x u i", x=4, u=2),
+                in_=src[:].rearrange("p t c -> p (t c)").bitcast(F32).rearrange("p (x i u) -> p x u i", x=4, u=2),
+            )
+            return x
+
+        def halve_act(g, s, b, engine):
+            act_raw[g, s, b] = halve(act_raw[g, s, b], f"hv{g}{s}{b}", engine)
+            turned.add((g, s, b))
+
+        def halve_pool(b, engine):
+            pl_val[b] = halve(pl_val[b], f"hvp{b}", engine)
+            turned.add(b)
+
+        def turn_words(bank, src, k, halved):
+            words = src[:].rearrange("p t c -> p (t c)").bitcast(F32)
+            for t in range(2):
+                for u in range(2):
+                    first = 512 * t + 256 * k
+                    if halved:
+                        picked = words[:, first + P * u : first + P * (u + 1)]
+                    else:
+                        picked = words[:, first + u : first + u + 255 : 2]
+                    nc.tensor.transpose(bank[:, 2 * t + u, :], picked, ident[:])
 
         def copy_words(bank, grp, lo, engine):
             copy = nc.vector.tensor_copy if engine == "v" else nc.scalar.copy
@@ -91,18 +121,14 @@ def tile_two_writer_residual_s8_kernel(
 
         def turn_act(g, k, b, engine="s"):
             bank = psum.tile([P, 4, P], F32, name=f"tr{g}{k}{b}", tag="bank", bufs=8)
-            words = act_raw[g, k // 2, b][:].rearrange("p t c -> p (t c)").bitcast(F32)
-            for t in range(2):
-                for u in range(2):
-                    first = 512 * t + 256 * (k % 2) + u
-                    nc.tensor.transpose(bank[:, 2 * t + u, :], words[:, first : first + 255 : 2], ident[:])
+            turn_words(bank, act_raw[g, k // 2, b], k % 2, (g, k // 2, b) in turned)
             if g == 1:
-                grp = ring.tile([P, 256, 4], BF16, name=f"ah{k}{b}", tag="grph", bufs=4, align_bytes=64)
+                grp = ring.tile([P, 256, 4], BF16, name=f"ah{k}{b}", tag="grp", bufs=9, align_bytes=64)
                 act_grp[g, k, b] = grp
                 lo = 0
             else:
                 if (g, k) not in act_grp:
-                    act_grp[g, k] = ring.tile([P, 512, 4], BF16, name=f"ag{g}{k}", tag="grp", bufs=4, align_bytes=64)
+                    act_grp[g, k] = ring.tile([P, 512, 4], BF16, name=f"ag{g}{k}", tag="grp", bufs=9, align_bytes=64)
                 grp = act_grp[g, k]
                 lo = 512 * b
             copy_words(bank, grp, lo, engine)
@@ -126,7 +152,7 @@ def tile_two_writer_residual_s8_kernel(
                 act_q[1, k, 2 * b + t] = stationary(q, t)
 
         def interleave(label, src, v_cols=V_COLS):
-            x = ring.tile([P, 512, 4], BF16, name=label, tag="wgrp", bufs=3, align_bytes=64)
+            x = ring.tile([P, 512, 4], BF16, name=label, tag="grp", bufs=9, align_bytes=64)
             for copy, lo, hi in ((nc.vector.tensor_copy, 0, v_cols), (nc.scalar.copy, v_cols, 512)):
                 if lo < hi:
                     copy(
@@ -175,8 +201,8 @@ def tile_two_writer_residual_s8_kernel(
                 for u in range(2):
                     first = 256 * (2 * b + t) + P * u
                     nc.tensor.transpose(bank[:, 2 * t + u, :], words[:, first : first + P], ident[:])
-            if b == 0:
-                ht_grp[g, n] = ring.tile([P, 512, 4], BF16, name=f"hg{g}{n}", tag="grp", bufs=4, align_bytes=64)
+            if (g, n) not in ht_grp:
+                ht_grp[g, n] = ring.tile([P, 512, 4], BF16, name=f"hg{g}{n}", tag="grp", bufs=9, align_bytes=64)
             copy_words(bank, ht_grp[g, n], 512 * b, engine)
 
         def quant_ht(g, n):
@@ -197,27 +223,23 @@ def tile_two_writer_residual_s8_kernel(
 
         def scale_pool(j):
             if j % 2 == 0:
-                pl_val[j // 2] = ring.tile([P, 2, M], BF16, name=f"pv{j}", tag="act", bufs=6, align_bytes=64)
+                pl_val[j // 2] = ring.tile([P, 2, M], BF16, name=f"pv{j}", tag="raw", bufs=10, align_bytes=64)
             nc.vector.tensor_tensor(
                 out=pl_val[j // 2][:, j % 2, :], in0=pl_raw[:, j, :].bitcast(FP8), in1=pl_scale[:], op=MULT
             )
 
         def turn_pool(k, b, engine="s"):
             bank = psum.tile([P, 4, P], F32, name=f"pt{k}{b}", tag="bank", bufs=8)
-            words = pl_val[b][:].rearrange("p j c -> p (j c)").bitcast(F32)
-            for t in range(2):
-                for u in range(2):
-                    first = 512 * t + 256 * k + u
-                    nc.tensor.transpose(bank[:, 2 * t + u, :], words[:, first : first + 255 : 2], ident[:])
+            turn_words(bank, pl_val[b], k, b in turned)
             if k not in pl_grp:
-                pl_grp[k] = ring.tile([P, 512, 4], BF16, name=f"pg{k}", tag="grp", bufs=4, align_bytes=64)
+                pl_grp[k] = ring.tile([P, 512, 4], BF16, name=f"pg{k}", tag="grp", bufs=9, align_bytes=64)
             copy_words(bank, pl_grp[k], 512 * b, engine)
 
         def quant_pool(k):
             pl_q[k] = quantize(f"pq{k}", pl_grp[k][:])
 
         def project(g, t, engines):
-            x = ring.tile([P, V], F32, name=f"yo{g}{t}", tag="out", bufs=6, align_bytes=64)
+            x = ring.tile([P, V], F32, name=f"yo{g}{t}", tag="out", bufs=5, align_bytes=64)
             for n in range(2):
                 cols = slice(HALF * n, HALF * (n + 1))
                 bank = psum.tile([P, HALF], F32, name=f"y{g}{t}{n}", tag="bank", bufs=8)
@@ -237,7 +259,7 @@ def tile_two_writer_residual_s8_kernel(
             bank = psum.tile([P, HALF], F32, name=f"c{n}{j}", tag="bank", bufs=8)
             for g in range(2):
                 mx(bank[:], stationary(pl_q[g], j), moving(hc_q[g, n]), g == 0, g == 1)
-            x = ring.tile([P, HALF], F32, name=f"co{n}{j}", tag="out", bufs=6, align_bytes=64)
+            x = ring.tile([P, HALF], F32, name=f"co{n}{j}", tag="out", bufs=5, align_bytes=64)
             dst = x[:].rearrange("p (k u e) -> p k u e", u=2, e=2)
             src = bank[:].rearrange("p (u k e) -> p k u e", u=2, e=2)
             if engine == "v":
@@ -284,185 +306,186 @@ def tile_two_writer_residual_s8_kernel(
 
         ALL, LOW, HIGH = range(4), range(2), range(2, 4)
 
-        load_act(0, 0, 1)
-        warm(14)
-        warm(8)
-        load_act(0, 0, 0)
-        warm(17)
-        warm(18)
-        load_act(1, 0, 1)
-        turn_pair(0, 0, 1, "sv")
-        turn_pair(0, 0, 0, "sv")
-        load_act(0, 2, 0)
-        load_w(0, 0)
-        load_w(0, 1)
-        turn_pair(1, 0, 1, "vs")
+        load_act(1, 2, 0)
         load_act(1, 0, 0)
-        quant_pair1(0, 1)
-        load_act(0, 2, 1)
+        load_w(0, 0)
+        halve_act(1, 2, 0, "v")
+        turn_pair(1, 2, 0, "ss")
+        load_act(1, 0, 1)
+        halve_act(1, 0, 0, "v")
+        group_w(0, 0, 320)
         load_act(1, 1, 0)
-        warm(19)
-        warm(6)
-        group_w(0, 0, 192)
-        group_w(0, 1, 384)
-        turn_pair(0, 2, 0, "ss")
-        quant_act(0)
-        warm(1)
-        load_act(1, 2, 1)
+        turn_pair(1, 0, 0, "sv")
         load_act(1, 1, 1)
         quant_w(0, 0)
-        warm(20)
-        turn_pair(1, 0, 0, "sv")
-        quant_w(0, 1)
-        quant_pair1(0, 0)
-        load_w(0, 3)
-        turn_pair(0, 2, 1, "ss")
-        sweep(1, 0, 0, HIGH)
-        load_act(1, 2, 0)
-        load_act(0, 1, 1)
-        load_act(0, 1, 0)
-        quant_act(1)
-        turn_pair(1, 1, 0, "sv")
-        warm(22)
-        load_w(0, 2)
-        load_w(1, 0)
+        load_act(0, 0, 0)
         warm(11)
-        turn_pair(1, 2, 1, "vs")
-        quant_pair1(1, 0)
+        load_w(0, 1)
+        warm(4)
+        quant_pair1(0, 0)
+        load_act(0, 2, 0)
+        load_act(0, 1, 1)
+        load_w(0, 2)
+        turn_pair(1, 0, 1, "sv")
+        load_act(0, 0, 1)
+        quant_pair1(0, 1)
+        warm(19)
+        load_act(0, 2, 1)
+        warm(10)
+        halve_act(0, 0, 0, "s")
+        quant_pair1(2, 0)
+        load_w(0, 3)
+        turn_pair(1, 1, 0, "ss")
+        group_w(0, 1, 256)
         sweep(1, 0, 0, LOW)
-        quant_pair1(2, 1)
-        turn_pair(1, 1, 1, "vs")
-        turn_pair(1, 2, 0, "ss")
+        turn_pair(1, 1, 1, "vv")
+        turn_pair(0, 0, 0, "ss")
+        load_act(0, 1, 0)
+        quant_w(0, 1)
+        warm(5)
+        quant_pair1(1, 1)
+        warm(17)
+        load_act(1, 2, 1)
+        turn_pair(0, 2, 0, "sv")
+        group_w(0, 2, 256)
+        turn_pair(0, 1, 1, "vs")
+        quant_w(0, 2)
+        sweep(1, 0, 0, HIGH)
+        quant_pair1(1, 0)
         sweep(1, 0, 1, LOW)
-        group_w(0, 3, 512)
         sweep(1, 0, 1, HIGH)
+        turn_pair(0, 0, 1, "sv")
+        turn_pair(0, 2, 1, "ss")
+        load_w(0, 4)
+        load_w(1, 1)
+        sweep(1, 0, 2, HIGH)
+        load_w(0, 5)
+        quant_act(0)
+        warm(21)
+        sweep(1, 0, 2, LOW)
+        group_w(0, 3, 320)
         quant_act(4)
         quant_w(0, 3)
-        quant_pair1(1, 1)
-        turn_pair(0, 1, 1, "ss")
-        load_w(0, 4)
-        group_w(0, 2, 384)
-        turn_pair(0, 1, 0, "sv")
-        load_w(0, 5)
-        quant_w(0, 2)
-        group_w(1, 0, 128)
-        quant_act(2)
-        quant_pair1(2, 0)
-        quant_act(3)
-        quant_w(1, 0)
-        sweep(0, 0, 0, ALL)
-        load_w(1, 2)
-        load_w(1, 1)
-        group_w(0, 4, 192)
-        sweep(0, 0, 1, ALL)
-        load_w(1, 3)
-        sweep(1, 0, 2, HIGH)
-        sweep(0, 0, 2, ALL)
-        sweep(1, 0, 3, HIGH)
-        sweep(1, 0, 2, LOW)
-        group_w(0, 5, 128)
-        quant_w(0, 4)
+        load_w(1, 0)
         quant_act(5)
-        load_res(0, 0)
-        sweep(0, 0, 3, ALL)
+        turn_pair(0, 1, 0, "ss")
+        turn_pair(1, 2, 1, "ss")
+        quant_act(2)
+        sweep(1, 0, 3, HIGH)
+        sweep(0, 0, 0, ALL)
+        quant_act(1)
+        quant_act(3)
+        group_w(0, 4, 192)
+        quant_pair1(2, 1)
+        quant_w(0, 4)
         sweep(1, 0, 3, LOW)
-        quant_w(0, 5)
-        sweep(0, 0, 4, ALL)
-        load_w(1, 4)
-        sweep(0, 0, 5, ALL)
-        group_w(1, 1, 512)
-        sweep(1, 0, 4, LOW)
-        sweep(1, 0, 5, LOW)
+        sweep(0, 0, 1, ALL)
+        group_w(1, 1, 384)
+        load_w(1, 2)
+        sweep(0, 0, 2, ALL)
+        group_w(0, 5, 256)
         sweep(1, 0, 4, HIGH)
-        load_pool()
-        sweep(1, 0, 5, HIGH)
-        quant_w(1, 1)
-        sweep(0, 1, 0, ALL)
-        sweep(0, 1, 1, ALL)
-        group_w(1, 2, 128)
-        add_pair(0, 0, 0)
-        add_pair(0, 0, 1)
+        sweep(0, 0, 3, ALL)
+        group_w(1, 0, 256)
+        sweep(1, 0, 4, LOW)
         load_res(1, 0)
-        load_w(1, 5)
-        load_pool_scale()
-        quant_w(1, 2)
-        group_w(1, 3, 192)
-        group_w(1, 4, 0)
-        load_res(1, 1)
+        quant_w(0, 5)
+        load_w(1, 3)
+        quant_w(1, 0)
+        quant_w(1, 1)
+        sweep(1, 0, 5, LOW)
+        sweep(1, 0, 5, HIGH)
         add_pair(1, 0, 1)
-        sweep(0, 1, 2, ALL)
-        group_w(1, 5, 0)
-        sweep(1, 1, 0, LOW)
-        quant_w(1, 3)
         add_pair(1, 0, 0)
-        load_wp()
-        sweep(1, 1, 1, LOW)
-        quant_w(1, 4)
-        group_hc(0, 0, 0)
-        quant_w(1, 5)
-        scale_pool(2)
-        scale_pool(3)
-        sweep(0, 1, 3, ALL)
-        sweep(1, 1, 2, LOW)
+        group_w(1, 2, 0)
+        load_w(1, 4)
+        group_w(1, 3, 192)
+        load_w(1, 5)
+        sweep(0, 0, 4, ALL)
+        load_res(0, 0)
+        sweep(0, 0, 5, ALL)
         load_res(0, 1)
+        sweep(0, 1, 0, ALL)
+        group_w(1, 4, 192)
+        sweep(0, 1, 1, ALL)
+        quant_w(1, 2)
+        quant_w(1, 3)
+        group_w(1, 5, 0)
+        sweep(0, 1, 2, ALL)
+        load_pool_scale()
+        quant_w(1, 4)
+        add_pair(0, 0, 1)
+        quant_w(1, 5)
+        sweep(0, 1, 3, ALL)
         sweep(0, 1, 4, ALL)
-        sweep(1, 1, 3, LOW)
-        group_hc(1, 0, 192)
+        load_pool()
+        load_wp_sc()
+        sweep(1, 1, 0, HIGH)
         sweep(0, 1, 5, ALL)
+        add_pair(0, 0, 0)
+        load_wp()
+        sweep(1, 1, 0, LOW)
         add_pair(0, 1, 0)
         add_pair(0, 1, 1)
-        turn_pool(0, 1, "v")
-        turn_pool(1, 1, "s")
-        sweep(1, 1, 4, LOW)
-        sweep(1, 1, 0, HIGH)
-        turn_h(0, 1, 0, "s")
-        turn_h(0, 1, 1, "s")
+        group_hc(1, 0, 0)
+        sweep(1, 1, 1, LOW)
+        group_hc(0, 0, 0)
+        group_hc(0, 1, 320)
+        quant_hc(0, 0)
+        sweep(1, 1, 1, HIGH)
         scale_pool(0)
         scale_pool(1)
+        sweep(1, 1, 2, HIGH)
+        scale_pool(2)
+        scale_pool(3)
+        turn_h(0, 1, 0, "s")
+        turn_h(0, 1, 1, "s")
         turn_h(0, 0, 0, "s")
         turn_h(0, 0, 1, "s")
-        sweep(1, 1, 5, LOW)
-        add_pair(1, 1, 0)
-        sweep(1, 1, 1, HIGH)
-        turn_h(1, 0, 0, "s")
-        turn_h(1, 0, 1, "s")
-        group_hc(0, 1, 256)
+        sweep(1, 1, 3, HIGH)
+        sweep(1, 1, 2, LOW)
+        sweep(1, 1, 3, LOW)
         quant_ht(0, 0)
+        sweep(1, 1, 4, HIGH)
         quant_ht(0, 1)
+        sweep(1, 1, 4, LOW)
+        quant_hc(1, 0)
+        load_res(1, 1)
+        sweep(1, 1, 5, LOW)
+        sweep(1, 1, 5, HIGH)
+        halve_pool(0, "s")
+        warm(0)
         turn_pool(0, 0, "s")
         turn_pool(1, 0, "s")
-        quant_hc(1, 0)
-        quant_pool(0)
-        turn_h(1, 1, 0, "s")
-        quant_hc(0, 0)
-        quant_hc(0, 1)
-        sweep(1, 1, 2, HIGH)
-        sweep(1, 1, 3, HIGH)
-        load_wp_sc()
-        quant_ht(1, 0)
-        quant_ht_pair(1, 1, 0)
-        project(0, 0, "ss")
-        sweep(1, 1, 4, HIGH)
+        turn_pool(0, 1, "v")
+        turn_pool(1, 1, "s")
+        project(0, 1, "ss")
         quant_pool(1)
-        project(0, 2, "ss")
-        project(0, 3, "vs")
-        sweep(1, 1, 5, HIGH)
-        pooled(0, 3, "s")
+        project(0, 3, "ss")
+        quant_pool(0)
+        add_pair(1, 1, 0)
         add_pair(1, 1, 1)
-        pooled(0, 2, "v")
-        group_hc(1, 1, 512)
-        project(1, 0, "ss")
-        project(0, 1, "sv")
-        project(1, 1, "sv")
-        turn_h(1, 1, 1, "s")
-        quant_hc(1, 1)
-        quant_ht_pair(1, 1, 1)
+        project(0, 2, "ss")
+        project(0, 0, "ss")
+        quant_hc(0, 1)
+        turn_h(1, 0, 0, "s")
+        turn_h(1, 0, 1, "v")
+        turn_h(1, 1, 1, "v")
+        turn_h(1, 1, 0, "s")
+        pooled(0, 3, "s")
+        pooled(0, 0, "s")
+        quant_ht(1, 0)
         pooled(0, 1, "s")
-        pooled(0, 0, "v")
-        pooled(1, 3, "s")
-        project(1, 3, "vs")
-        pooled(1, 2, "s")
+        quant_ht_pair(1, 1, 1)
+        group_hc(1, 1, 512)
+        quant_ht_pair(1, 1, 0)
+        quant_hc(1, 1)
+        project(1, 3, "ss")
         project(1, 2, "sv")
-        warm(3)
+        pooled(0, 2, "s")
+        pooled(1, 1, "v")
+        project(1, 1, "sv")
+        project(1, 0, "sv")
         pooled(1, 0, "s")
-        pooled(1, 1, "s")
+        pooled(1, 3, "s")
+        pooled(1, 2, "s")

@@ -15,13 +15,21 @@ ADD = mybir.AluOpType.add
 MULT = mybir.AluOpType.mult
 
 P = 128
-M, H, F, D, V, R = 1024, 1024, 2048, 1024, 1024, 512
-FLOPS = 2 * M * D * (H + F) + 2 * M * D * V + 2 * R * M * D
+COLS = 512
+TOKENS, SLOTS = 1024, 512
+ATTN_WIDTH, MLP_WIDTH, RESIDUAL_WIDTH, PROJECTION_WIDTH = 1024, 2048, 1024, 1024
+FLOPS = 2 * TOKENS * RESIDUAL_WIDTH * (ATTN_WIDTH + MLP_WIDTH + PROJECTION_WIDTH + SLOTS)
 
-HALF = 512
-KA, KM = H // 512, F // 512
-PASSES = KA + KM
-V_COLS = 320
+ATTN_PASSES = ATTN_WIDTH // 512
+PASSES = (ATTN_WIDTH + MLP_WIDTH) // 512
+ALL, LOW, HIGH = range(4), range(2), range(2, 4)
+
+NARROW_BUFS = 11
+MLP_BUFS = 3
+SORTED_BUFS = 2
+GROUPED_BUFS = 9
+COLUMN_CODE_BUFS = 12
+BANKS = 8
 
 
 def tile_two_writer_residual_s8_kernel(
@@ -31,146 +39,139 @@ def tile_two_writer_residual_s8_kernel(
     with ExitStack() as ctx:
         keep = ctx.enter_context(tc.tile_pool(name="keep", bufs=1))
         ring = ctx.enter_context(tc.tile_pool(name="ring", bufs=2))
-        psum = ctx.enter_context(tc.psum_pool(name="psum", bufs=4))
+        psum = ctx.enter_context(tc.psum_pool(name="psum", bufs=BANKS))
 
         def kept(label, shape, dtype):
             return keep.tile(shape, dtype, name=label, tag=label, bufs=1, align_bytes=64)
 
+        def grouped(label, columns):
+            return ring.tile([P, columns, 4], BF16, name=label, tag="grouped", bufs=GROUPED_BUFS, align_bytes=64)
+
+        def bank_of(label, shape):
+            return psum.tile(shape, F32, name=label, tag="bank", bufs=BANKS)
+
         ident = kept("ident", [P, P], F32)
-        wp_sc = kept("wp_sc", [P, 2, V], U8)
-        zeros = kept("zeros", [P, 512], BF16)
+        wp_plane = kept("wp_plane", [P, 2, PROJECTION_WIDTH], U8)
+        zeros = kept("zeros", [P, COLS], BF16)
         nc.vector.memset(zeros[:], 0.0)
         make_identity(nc, ident[:])
-        nc.gpsimd.memset(wp_sc[:].rearrange("p g n -> p (g n)").bitcast(I32), 0)
+        nc.gpsimd.memset(wp_plane[:].rearrange("p g n -> p (g n)").bitcast(I32), 0)
 
         ctx.enter_context(tc.manual_schedule())
 
-        attn_v = attn.rearrange("(g p t) k -> g p t k", p=P, t=4)
-        mlp_v = mlp.rearrange("(g p t) k -> g p t k", p=P, t=4)
-        resid_v = resid.rearrange("(g p t) d -> g p t d", p=P, t=4)
-        wo_v = wo.rearrange("(k p j) d -> k p j d", p=P, j=4)
-        wd_v = wd.rearrange("(k p j) d -> k p j d", p=P, j=4)
-        y_v = out_0.rearrange("(g p t) v -> g t p v", p=P, t=4)
-        c_v = out_1.rearrange("(p j) d -> j p d", j=4)
+        attn_rows = attn.rearrange("(g p t) k -> g p t k", p=P, t=4)
+        mlp_rows = mlp.rearrange("(g p t) k -> g p t k", p=P, t=4)
+        resid_rows = resid.rearrange("(g p t) d -> g p t d", p=P, t=4)
+        wo_rows = wo.rearrange("(k p j) d -> k p j d", p=P, j=4)
+        wd_rows = wd.rearrange("(k p j) d -> k p j d", p=P, j=4)
+        y_rows = out_0.rearrange("(g p t) v -> g t p v", p=P, t=4)
+        c_rows = out_1.rearrange("(p j) d -> j p d", j=4)
 
-        act_raw, act_grp, act_q = {}, {}, {}
-        w_raw, w_grp, w_q = {}, {}, {}
-        res, acc, h, ht_grp, ht_q, hc_grp, hc_q = {}, {}, {}, {}, {}, {}, {}
-        pl_val, pl_grp, pl_q = {}, {}, {}
+        act_words, act_grouped, act_operand = {}, {}, {}
+        weight_raw, weight_grouped, weight_operand = {}, {}, {}
+        resid_half, total, h = {}, {}, {}
+        h_row_grouped, h_row_operand, h_token_grouped, h_token_operand = {}, {}, {}, {}
+        pool_value, pool_words, pool_grouped, pool_operand = {}, {}, {}, {}
+        sorted_units = set()
 
-        def load_act(g, s, b):
-            x = ring.tile([P, 2, 1024], BF16, name=f"act{g}{s}{b}", tag="raw", bufs=10, align_bytes=64)
-            two = slice(2 * b, 2 * b + 2)
-            if s == 0:
-                nc.sync.dma_start(out=x[:], in_=attn_v[g][:, two, :])
-            else:
-                nc.sync.dma_start(out=x[:], in_=mlp_v[g][:, two, 1024 * (s - 1) : 1024 * s])
-            act_raw[g, s, b] = x
+        wp = kept("wp", [P, 2, 2 * PROJECTION_WIDTH], U8)
+        pool_raw = kept("pool_raw", [P, 4, TOKENS], U8)
+        scale_row = kept("scale_row", [P, TOKENS], F32)
 
-        def load_w(n, k):
-            x = ring.tile([P, 4, HALF], BF16, name=f"w{n}{k}", tag="raw", bufs=10, align_bytes=64)
-            rows = wo_v[k] if k < KA else wd_v[k - KA]
-            nc.sync.dma_start(out=x[:], in_=rows[:, :, HALF * n : HALF * (n + 1)])
-            w_raw[n, k] = x
+        def load_attn(g, b):
+            x = ring.tile([P, 2, ATTN_WIDTH], BF16, name=f"attn{g}{b}", tag="narrow", bufs=NARROW_BUFS, align_bytes=64)
+            nc.sync.dma_start(out=x[:], in_=attn_rows[g][:, 2 * b : 2 * b + 2, :])
+            act_words[g, 0, b] = x[:].bitcast(F32)
 
-        def load_res(g, n):
-            res[g, n] = kept(f"res{g}{n}", [P, 4, HALF], BF16)
-            nc.sync.dma_start(out=res[g, n][:], in_=resid_v[g][:, :, HALF * n : HALF * (n + 1)])
+        def load_mlp(g, b):
+            x = ring.tile([P, 2, MLP_WIDTH], BF16, name=f"mlp{g}{b}", tag="mlp", bufs=MLP_BUFS, align_bytes=64)
+            nc.sync.dma_start(out=x[:], in_=mlp_rows[g][:, 2 * b : 2 * b + 2, :])
+            for s in (1, 2):
+                act_words[g, s, b] = x[:, :, 1024 * (s - 1) : 1024 * s].bitcast(F32)
 
-        turned = set()
+        def load_weights(n, k):
+            x = ring.tile([P, 4, COLS], BF16, name=f"w{n}{k}", tag="narrow", bufs=NARROW_BUFS, align_bytes=64)
+            rows = wo_rows[k] if k < ATTN_PASSES else wd_rows[k - ATTN_PASSES]
+            nc.sync.dma_start(out=x[:], in_=rows[:, :, COLS * n : COLS * (n + 1)])
+            weight_raw[n, k] = x
 
-        def halve(src, label, engine):
-            x = ring.tile([P, 2, 1024], BF16, name=label, tag="halves", bufs=2, align_bytes=64)
-            copy = nc.vector.tensor_copy if engine == "v" else nc.scalar.copy
-            copy(
-                out=x[:].rearrange("p t c -> p (t c)").bitcast(F32).rearrange("p (x u i) -> p x u i", x=4, u=2),
-                in_=src[:].rearrange("p t c -> p (t c)").bitcast(F32).rearrange("p (x i u) -> p x u i", x=4, u=2),
-            )
-            return x
+        def load_resid(g, n):
+            resid_half[g, n] = kept(f"resid{g}{n}", [P, 4, COLS], BF16)
+            nc.sync.dma_start(out=resid_half[g, n][:], in_=resid_rows[g][:, :, COLS * n : COLS * (n + 1)])
 
-        def halve_act(g, s, b, engine):
-            act_raw[g, s, b] = halve(act_raw[g, s, b], f"hv{g}{s}{b}", engine)
-            turned.add((g, s, b))
+        def load_wp():
+            nc.sync.dma_start(out=wp[:], in_=wp_words.rearrange("g p n -> p g n"))
 
-        def halve_pool(b, engine):
-            pl_val[b] = halve(pl_val[b], f"hvp{b}", engine)
-            turned.add(b)
+        def load_wp_scales():
+            for q in range(4):
+                nc.sync.dma_start(
+                    out=wp_plane[32 * q : 32 * q + 4].bitcast(I32),
+                    in_=wp_scales[:, 4 * q : 4 * q + 4, :].rearrange("g r n -> r g n").bitcast(I32),
+                )
 
-        def turn_words(bank, src, k, halved):
-            words = src[:].rearrange("p t c -> p (t c)").bitcast(F32)
-            for t in range(2):
+        def load_pool_bytes():
+            nc.sync.dma_start(out=pool_raw[:], in_=pool_bytes.rearrange("(p j) m -> p j m", j=4))
+
+        def load_pool_scale():
+            nc.sync.dma_start(out=scale_row[:], in_=pool_scale.rearrange("o m -> (o m)").partition_broadcast(P))
+
+        def warm(i):
+            bank = bank_of(f"warm{i}", [P, COLS])
+            nc.tensor.matmul(bank[:], lhsT=zeros[:, :P], rhs=zeros[:], start=True, stop=True)
+
+        def copy_by(engine):
+            return nc.vector.tensor_copy if engine == "v" else nc.scalar.copy
+
+        def sort_words(words, label, engine):
+            x = ring.tile([P, 2, 1024], BF16, name=label, tag="sorted", bufs=SORTED_BUFS, align_bytes=64)
+            in_order = x[:].bitcast(F32)
+            for r in range(2):
+                copy_by(engine)(
+                    out=in_order[:, r, :].rearrange("p (k u i) -> p k u i", k=2, u=2),
+                    in_=words[:, r, :].rearrange("p (k i u) -> p k u i", k=2, u=2),
+                )
+            return in_order
+
+        def transpose_words(bank, words, i, in_order):
+            for r in range(2):
                 for u in range(2):
-                    first = 512 * t + 256 * k
-                    if halved:
-                        picked = words[:, first + P * u : first + P * (u + 1)]
+                    if in_order:
+                        picked = words[:, r, 256 * i + P * u : 256 * i + P * (u + 1)]
                     else:
-                        picked = words[:, first + u : first + u + 255 : 2]
-                    nc.tensor.transpose(bank[:, 2 * t + u, :], picked, ident[:])
+                        picked = words[:, r, 256 * i + u : 256 * i + u + 255 : 2]
+                    nc.tensor.transpose(bank[:, 2 * r + u, :], picked, ident[:])
 
-        def copy_words(bank, grp, lo, engine):
-            copy = nc.vector.tensor_copy if engine == "v" else nc.scalar.copy
-            dst = grp[:].rearrange("p r j -> p (r j)").bitcast(F32)
-            copy(
-                out=dst[:, lo : lo + 512].rearrange("p (t r u) -> p t r u", t=2, u=2),
+        def empty_words(bank, x, first, engine):
+            dst = x[:].rearrange("p r j -> p (r j)").bitcast(F32)
+            copy_by(engine)(
+                out=dst[:, first : first + COLS].rearrange("p (t r u) -> p t r u", t=2, u=2),
                 in_=bank[:].rearrange("p (t u) r -> p t r u", u=2),
             )
 
-        def warm(i):
-            bank = psum.tile([P, HALF], F32, name=f"warm{i}", tag="bank", bufs=8)
-            nc.tensor.matmul(bank[:], lhsT=zeros[:, :P], rhs=zeros[:], start=True, stop=True)
+        def sort_act(g, s, b, engine):
+            act_words[g, s, b] = sort_words(act_words[g, s, b], f"sorted{g}{s}{b}", engine)
+            sorted_units.add((g, s, b))
 
-        def turn_act(g, k, b, engine="s"):
-            bank = psum.tile([P, 4, P], F32, name=f"tr{g}{k}{b}", tag="bank", bufs=8)
-            turn_words(bank, act_raw[g, k // 2, b], k % 2, (g, k // 2, b) in turned)
-            if g == 1:
-                grp = ring.tile([P, 256, 4], BF16, name=f"ah{k}{b}", tag="grp", bufs=9, align_bytes=64)
-                act_grp[g, k, b] = grp
-                lo = 0
+        def turn_act(g, s, b, engines):
+            for i in range(2):
+                k = 2 * s + i
+                bank = bank_of(f"turn{g}{k}{b}", [P, 4, P])
+                transpose_words(bank, act_words[g, s, b], i, (g, s, b) in sorted_units)
+                unit = (g, k) if g == 0 else (g, k, b)
+                if unit not in act_grouped:
+                    act_grouped[unit] = grouped(f"act{g}{k}{b}", 512 if g == 0 else 256)
+                empty_words(bank, act_grouped[unit], COLS * b if g == 0 else 0, engines[i])
+
+        def quantize(label, x, columns, streams=False):
+            if streams:
+                bufs = COLUMN_CODE_BUFS
+                codes = ring.tile([P, columns], U32, name=label + "_codes", tag="codes", bufs=bufs, align_bytes=64)
+                plane = ring.tile([P, columns], U8, name=label + "_plane", tag="plane", bufs=bufs, align_bytes=64)
             else:
-                if (g, k) not in act_grp:
-                    act_grp[g, k] = ring.tile([P, 512, 4], BF16, name=f"ag{g}{k}", tag="grp", bufs=9, align_bytes=64)
-                grp = act_grp[g, k]
-                lo = 512 * b
-            copy_words(bank, grp, lo, engine)
-
-        def quantize(label, grp, width=512):
-            codes = kept(label + "_c", [P, width], U32)
-            scales = kept(label + "_s", [P, width], U8)
-            nc.vector.quantize_mx(
-                out=codes[:].bitcast(FP8X4), scales=scales[:], in_=grp.rearrange("p c j -> p (c j)")
-            )
-            return codes, scales
-
-        def quant_act(k):
-            q = quantize(f"aq{k}", act_grp[0, k][:])
-            for t in range(4):
-                act_q[0, k, t] = stationary(q, t)
-
-        def quant_act1(k, b):
-            q = quantize(f"ar{k}{b}", act_grp[1, k, b][:], 256)
-            for t in range(2):
-                act_q[1, k, 2 * b + t] = stationary(q, t)
-
-        def interleave(label, src, v_cols=V_COLS):
-            x = ring.tile([P, 512, 4], BF16, name=label, tag="grp", bufs=9, align_bytes=64)
-            for copy, lo, hi in ((nc.vector.tensor_copy, 0, v_cols), (nc.scalar.copy, v_cols, 512)):
-                if lo < hi:
-                    copy(
-                        out=x[:, lo:hi, :].rearrange("p (c i) j -> p c j i", i=4),
-                        in_=src[:, :, lo:hi].rearrange("p j (c i) -> p c j i", i=4),
-                    )
-            return x
-
-        def group_w(n, k, v_cols):
-            w_grp[n, k] = interleave(f"wg{n}{k}", w_raw[n, k], v_cols)
-
-        def quant_w(n, k):
-            w_q[n, k] = quantize(f"wq{n}{k}", w_grp[n, k][:])
-
-        def mx(out, a, b, start, stop):
-            nc.tensor.matmul_mx(
-                out=out, lhsT=a[0], lhsT_scale=a[1], rhs=b[0], rhs_scale=b[1], start=start, stop=stop
-            )
+                codes = kept(label + "_codes", [P, columns], U32)
+                plane = kept(label + "_plane", [P, columns], U8)
+            nc.vector.quantize_mx(out=codes[:].bitcast(FP8X4), scales=plane[:], in_=x.rearrange("p c j -> p (c j)"))
+            return codes, plane
 
         def stationary(q, t):
             cols = slice(P * t, P * (t + 1))
@@ -179,313 +180,302 @@ def tile_two_writer_residual_s8_kernel(
         def moving(q):
             return q[0][:].bitcast(FP8X4), q[1][:]
 
-        def write_stream(g, n, k, t):
-            if k == 0:
-                acc[g, n, t] = psum.tile([P, HALF], F32, name=f"acc{g}{n}{t}", tag="bank", bufs=8)
-            mx(acc[g, n, t][:], act_q[g, k, t], moving(w_q[n, k]), k == 0, k == PASSES - 1)
+        def quantize_act(k):
+            q = quantize(f"act0{k}", act_grouped[0, k][:], 512)
+            for t in ALL:
+                act_operand[0, k, t] = stationary(q, t)
 
-        def add_res(g, n, t):
+        def quantize_act_pair(s, b):
+            for k in (2 * s, 2 * s + 1):
+                q = quantize(f"act1{k}{b}", act_grouped[1, k, b][:], 256)
+                for t in range(2):
+                    act_operand[1, k, 2 * b + t] = stationary(q, t)
+
+        def interleave(label, rows, v_cols):
+            x = grouped(label, COLS)
+            for copy, lo, hi in ((nc.vector.tensor_copy, 0, v_cols), (nc.scalar.copy, v_cols, COLS)):
+                if lo < hi:
+                    copy(
+                        out=x[:, lo:hi, :].rearrange("p (c i) j -> p c j i", i=4),
+                        in_=rows[:, :, lo:hi].rearrange("p j (c i) -> p c j i", i=4),
+                    )
+            return x
+
+        def group_weights(n, k, v_cols):
+            weight_grouped[n, k] = interleave(f"w_grouped{n}{k}", weight_raw[n, k], v_cols)
+
+        def quantize_weights(n, k):
+            weight_operand[n, k] = moving(quantize(f"w{n}{k}", weight_grouped[n, k][:], COLS, streams=True))
+
+        def mx(out, a, b, start, stop):
+            nc.tensor.matmul_mx(out=out, lhsT=a[0], lhsT_scale=a[1], rhs=b[0], rhs_scale=b[1], start=start, stop=stop)
+
+        def write_stream(g, n, k, tiles):
+            for t in tiles:
+                if k == 0:
+                    total[g, n, t] = bank_of(f"total{g}{n}{t}", [P, COLS])
+                mx(total[g, n, t][:], act_operand[g, k, t], weight_operand[n, k], k == 0, k == PASSES - 1)
+
+        def add_resid(g, n, b):
             if (g, n) not in h:
-                h[g, n] = ring.tile([P, 4, HALF], BF16, name=f"h{g}{n}", tag="h", bufs=4, align_bytes=64)
-            nc.vector.tensor_tensor(
-                out=h[g, n][:, t, :].rearrange("p (u k e) -> p u k e", u=2, e=2),
-                in0=acc[g, n, t][:].rearrange("p (k u e) -> p u k e", u=2, e=2),
-                in1=res[g, n][:, t, :].rearrange("p (k u e) -> p u k e", u=2, e=2),
-                op=ADD,
-            )
-
-        def turn_h(g, n, b, engine="s"):
-            bank = psum.tile([P, 4, P], F32, name=f"ht{g}{n}{b}", tag="bank", bufs=8)
-            words = h[g, n][:].rearrange("p t c -> p (t c)").bitcast(F32)
-            for t in range(2):
-                for u in range(2):
-                    first = 256 * (2 * b + t) + P * u
-                    nc.tensor.transpose(bank[:, 2 * t + u, :], words[:, first : first + P], ident[:])
-            if (g, n) not in ht_grp:
-                ht_grp[g, n] = ring.tile([P, 512, 4], BF16, name=f"hg{g}{n}", tag="grp", bufs=9, align_bytes=64)
-            copy_words(bank, ht_grp[g, n], 512 * b, engine)
-
-        def quant_ht(g, n):
-            q = quantize(f"hq{g}{n}", ht_grp[g, n][:])
-            for t in range(4):
-                ht_q[g, n, t] = stationary(q, t)
-
-        def quant_ht_pair(g, n, b):
-            q = quantize(f"hq{g}{n}{b}", ht_grp[g, n][:, 256 * b : 256 * (b + 1), :], 256)
-            for t in range(2):
-                ht_q[g, n, 2 * b + t] = stationary(q, t)
-
-        def group_hc(g, n, v_cols=V_COLS):
-            hc_grp[g, n] = interleave(f"hcg{g}{n}", h[g, n], v_cols)
-
-        def quant_hc(g, n):
-            hc_q[g, n] = quantize(f"hcq{g}{n}", hc_grp[g, n][:])
-
-        def scale_pool(j):
-            if j % 2 == 0:
-                pl_val[j // 2] = ring.tile([P, 2, M], BF16, name=f"pv{j}", tag="raw", bufs=10, align_bytes=64)
-            nc.vector.tensor_tensor(
-                out=pl_val[j // 2][:, j % 2, :], in0=pl_raw[:, j, :].bitcast(FP8), in1=pl_scale[:], op=MULT
-            )
-
-        def turn_pool(k, b, engine="s"):
-            bank = psum.tile([P, 4, P], F32, name=f"pt{k}{b}", tag="bank", bufs=8)
-            turn_words(bank, pl_val[b], k, b in turned)
-            if k not in pl_grp:
-                pl_grp[k] = ring.tile([P, 512, 4], BF16, name=f"pg{k}", tag="grp", bufs=9, align_bytes=64)
-            copy_words(bank, pl_grp[k], 512 * b, engine)
-
-        def quant_pool(k):
-            pl_q[k] = quantize(f"pq{k}", pl_grp[k][:])
-
-        def project(g, t, engines):
-            x = ring.tile([P, V], F32, name=f"yo{g}{t}", tag="out", bufs=5, align_bytes=64)
-            for n in range(2):
-                cols = slice(HALF * n, HALF * (n + 1))
-                bank = psum.tile([P, HALF], F32, name=f"y{g}{t}{n}", tag="bank", bufs=8)
-                for k in range(2):
-                    w = (wp[:, k, 2 * HALF * n : 2 * HALF * (n + 1)].bitcast(FP4X4), wp_sc[:, k, cols])
-                    mx(bank[:], ht_q[g, k, t], w, k == 0, k == 1)
-                if engines[n] == "v":
-                    nc.vector.tensor_copy(out=x[:, cols], in_=bank[:])
-                else:
-                    nc.scalar.copy(out=x[:, cols], in_=bank[:])
-                if g == 1 and t == 3:
-                    nc.sync.dma_start(out=y_v[g, t][:, cols], in_=x[:, cols])
-            if not (g == 1 and t == 3):
-                nc.sync.dma_start(out=y_v[g, t], in_=x[:])
-
-        def pooled(n, j, engine):
-            bank = psum.tile([P, HALF], F32, name=f"c{n}{j}", tag="bank", bufs=8)
-            for g in range(2):
-                mx(bank[:], stationary(pl_q[g], j), moving(hc_q[g, n]), g == 0, g == 1)
-            x = ring.tile([P, HALF], F32, name=f"co{n}{j}", tag="out", bufs=5, align_bytes=64)
-            dst = x[:].rearrange("p (k u e) -> p k u e", u=2, e=2)
-            src = bank[:].rearrange("p (u k e) -> p k u e", u=2, e=2)
-            if engine == "v":
-                nc.vector.tensor_copy(out=dst, in_=src)
-            else:
-                nc.scalar.copy(out=dst, in_=src)
-            nc.sync.dma_start(out=c_v[j][:, HALF * n : HALF * (n + 1)], in_=x[:])
-
-        wp = kept("wp", [P, 2, 2 * V], U8)
-        pl_raw = kept("pl_raw", [P, 4, M], U8)
-        pl_scale = kept("pl_scale", [P, M], F32)
-
-        def load_wp():
-            nc.sync.dma_start(out=wp[:], in_=wp_words.rearrange("g p n -> p g n"))
-
-        def load_wp_sc():
-            for q in range(4):
-                nc.sync.dma_start(
-                    out=wp_sc[32 * q : 32 * q + 4].bitcast(I32),
-                    in_=wp_scales[:, 4 * q : 4 * q + 4, :].rearrange("g r n -> r g n").bitcast(I32),
+                h[g, n] = kept(f"h{g}{n}", [P, 4, COLS], BF16)
+            for t in (2 * b, 2 * b + 1):
+                nc.vector.tensor_tensor(
+                    out=h[g, n][:, t, :].rearrange("p (u i e) -> p u i e", u=2, e=2),
+                    in0=total[g, n, t][:].rearrange("p (i u e) -> p u i e", u=2, e=2),
+                    in1=resid_half[g, n][:, t, :].rearrange("p (i u e) -> p u i e", u=2, e=2),
+                    op=ADD,
                 )
 
-        def load_pool():
-            nc.sync.dma_start(out=pl_raw[:], in_=pool_bytes.rearrange("(p j) m -> p j m", j=4))
+        def turn_h(g, n, b, engine):
+            bank = bank_of(f"turn_h{g}{n}{b}", [P, 4, P])
+            words = h[g, n][:, 2 * b : 2 * b + 2, :].bitcast(F32)
+            transpose_words(bank, words, 0, True)
+            if (g, n) not in h_row_grouped:
+                h_row_grouped[g, n] = grouped(f"h_row{g}{n}", 512)
+            empty_words(bank, h_row_grouped[g, n], COLS * b, engine)
 
-        def load_pool_scale():
-            nc.sync.dma_start(out=pl_scale[:], in_=pool_scale.rearrange("o m -> (o m)").partition_broadcast(P))
+        def quantize_h_rows(g, n):
+            q = quantize(f"h_row{g}{n}", h_row_grouped[g, n][:], 512)
+            for t in ALL:
+                h_row_operand[g, n, t] = stationary(q, t)
 
-        def turn_pair(g, s, b, engines):
-            turn_act(g, 2 * s, b, engines[0])
-            turn_act(g, 2 * s + 1, b, engines[1])
+        def quantize_h_rows_pair(g, n, b):
+            q = quantize(f"h_row{g}{n}{b}", h_row_grouped[g, n][:, 256 * b : 256 * (b + 1), :], 256)
+            for t in range(2):
+                h_row_operand[g, n, 2 * b + t] = stationary(q, t)
 
-        def quant_pair1(s, b):
-            quant_act1(2 * s, b)
-            quant_act1(2 * s + 1, b)
+        def group_h_tokens(g, n, v_cols):
+            h_token_grouped[g, n] = interleave(f"h_token_grouped{g}{n}", h[g, n], v_cols)
 
-        def sweep(g, n, k, tiles):
-            for t in tiles:
-                write_stream(g, n, k, t)
+        def quantize_h_tokens(g, n):
+            h_token_operand[g, n] = moving(quantize(f"h_token{g}{n}", h_token_grouped[g, n][:], COLS, streams=True))
 
-        def add_pair(g, n, b):
-            add_res(g, n, 2 * b)
-            add_res(g, n, 2 * b + 1)
+        def scale_pool(b):
+            pool_value[b] = ring.tile([P, 2, TOKENS], BF16, name=f"pool{b}", tag="narrow", bufs=NARROW_BUFS, align_bytes=64)
+            pool_words[b] = pool_value[b][:].bitcast(F32)
+            for r in range(2):
+                nc.vector.tensor_tensor(
+                    out=pool_value[b][:, r, :],
+                    in0=pool_raw[:, 2 * b + r, :].bitcast(FP8),
+                    in1=scale_row[:],
+                    op=MULT,
+                )
 
-        ALL, LOW, HIGH = range(4), range(2), range(2, 4)
+        def sort_pool(b, engine):
+            pool_words[b] = sort_words(pool_words[b], f"sorted_pool{b}", engine)
+            sorted_units.add(b)
 
-        load_act(1, 2, 0)
-        load_act(1, 0, 0)
-        load_w(0, 0)
-        halve_act(1, 2, 0, "v")
-        turn_pair(1, 2, 0, "ss")
-        load_act(1, 0, 1)
-        halve_act(1, 0, 0, "v")
-        group_w(0, 0, 320)
-        load_act(1, 1, 0)
-        turn_pair(1, 0, 0, "sv")
-        load_act(1, 1, 1)
-        quant_w(0, 0)
-        load_act(0, 0, 0)
-        warm(11)
-        load_w(0, 1)
-        warm(4)
-        quant_pair1(0, 0)
-        load_act(0, 2, 0)
-        load_act(0, 1, 1)
-        load_w(0, 2)
-        turn_pair(1, 0, 1, "sv")
-        load_act(0, 0, 1)
-        quant_pair1(0, 1)
-        warm(19)
-        load_act(0, 2, 1)
-        warm(10)
-        halve_act(0, 0, 0, "s")
-        quant_pair1(2, 0)
-        load_w(0, 3)
-        turn_pair(1, 1, 0, "ss")
-        group_w(0, 1, 256)
-        sweep(1, 0, 0, LOW)
-        turn_pair(1, 1, 1, "vv")
-        turn_pair(0, 0, 0, "ss")
-        load_act(0, 1, 0)
-        quant_w(0, 1)
-        warm(5)
-        quant_pair1(1, 1)
-        warm(17)
-        load_act(1, 2, 1)
-        turn_pair(0, 2, 0, "sv")
-        group_w(0, 2, 256)
-        turn_pair(0, 1, 1, "vs")
-        quant_w(0, 2)
-        sweep(1, 0, 0, HIGH)
-        quant_pair1(1, 0)
-        sweep(1, 0, 1, LOW)
-        sweep(1, 0, 1, HIGH)
-        turn_pair(0, 0, 1, "sv")
-        turn_pair(0, 2, 1, "ss")
-        load_w(0, 4)
-        load_w(1, 1)
-        sweep(1, 0, 2, HIGH)
-        load_w(0, 5)
-        quant_act(0)
-        warm(21)
-        sweep(1, 0, 2, LOW)
-        group_w(0, 3, 320)
-        quant_act(4)
-        quant_w(0, 3)
-        load_w(1, 0)
-        quant_act(5)
-        turn_pair(0, 1, 0, "ss")
-        turn_pair(1, 2, 1, "ss")
-        quant_act(2)
-        sweep(1, 0, 3, HIGH)
-        sweep(0, 0, 0, ALL)
-        quant_act(1)
-        quant_act(3)
-        group_w(0, 4, 192)
-        quant_pair1(2, 1)
-        quant_w(0, 4)
-        sweep(1, 0, 3, LOW)
-        sweep(0, 0, 1, ALL)
-        group_w(1, 1, 384)
-        load_w(1, 2)
-        sweep(0, 0, 2, ALL)
-        group_w(0, 5, 256)
-        sweep(1, 0, 4, HIGH)
-        sweep(0, 0, 3, ALL)
-        group_w(1, 0, 256)
-        sweep(1, 0, 4, LOW)
-        load_res(1, 0)
-        quant_w(0, 5)
-        load_w(1, 3)
-        quant_w(1, 0)
-        quant_w(1, 1)
-        sweep(1, 0, 5, LOW)
-        sweep(1, 0, 5, HIGH)
-        add_pair(1, 0, 1)
-        add_pair(1, 0, 0)
-        group_w(1, 2, 0)
-        load_w(1, 4)
-        group_w(1, 3, 192)
-        load_w(1, 5)
-        sweep(0, 0, 4, ALL)
-        load_res(0, 0)
-        sweep(0, 0, 5, ALL)
-        load_res(0, 1)
-        sweep(0, 1, 0, ALL)
-        group_w(1, 4, 192)
-        sweep(0, 1, 1, ALL)
-        quant_w(1, 2)
-        quant_w(1, 3)
-        group_w(1, 5, 0)
-        sweep(0, 1, 2, ALL)
-        load_pool_scale()
-        quant_w(1, 4)
-        add_pair(0, 0, 1)
-        quant_w(1, 5)
-        sweep(0, 1, 3, ALL)
-        sweep(0, 1, 4, ALL)
-        load_pool()
-        load_wp_sc()
-        sweep(1, 1, 0, HIGH)
-        sweep(0, 1, 5, ALL)
-        add_pair(0, 0, 0)
-        load_wp()
-        sweep(1, 1, 0, LOW)
-        add_pair(0, 1, 0)
-        add_pair(0, 1, 1)
-        group_hc(1, 0, 0)
-        sweep(1, 1, 1, LOW)
-        group_hc(0, 0, 0)
-        group_hc(0, 1, 320)
-        quant_hc(0, 0)
-        sweep(1, 1, 1, HIGH)
-        scale_pool(0)
-        scale_pool(1)
-        sweep(1, 1, 2, HIGH)
-        scale_pool(2)
-        scale_pool(3)
-        turn_h(0, 1, 0, "s")
-        turn_h(0, 1, 1, "s")
-        turn_h(0, 0, 0, "s")
-        turn_h(0, 0, 1, "s")
-        sweep(1, 1, 3, HIGH)
-        sweep(1, 1, 2, LOW)
-        sweep(1, 1, 3, LOW)
-        quant_ht(0, 0)
-        sweep(1, 1, 4, HIGH)
-        quant_ht(0, 1)
-        sweep(1, 1, 4, LOW)
-        quant_hc(1, 0)
-        load_res(1, 1)
-        sweep(1, 1, 5, LOW)
-        sweep(1, 1, 5, HIGH)
-        halve_pool(0, "s")
+        def turn_pool(b, engines):
+            for k in range(2):
+                bank = bank_of(f"turn_pool{k}{b}", [P, 4, P])
+                transpose_words(bank, pool_words[b], k, b in sorted_units)
+                if k not in pool_grouped:
+                    pool_grouped[k] = grouped(f"pool_grouped{k}", SLOTS)
+                empty_words(bank, pool_grouped[k], COLS * b, engines[k])
+
+        def quantize_pool(k):
+            pool_operand[k] = quantize(f"pool{k}", pool_grouped[k][:], SLOTS)
+
+        def project(g, t, engines):
+            x = ring.tile([P, PROJECTION_WIDTH], F32, name=f"y{g}{t}", tag="narrow", bufs=NARROW_BUFS, align_bytes=64)
+            for i in range(2):
+                cols = slice(COLS * i, COLS * (i + 1))
+                bank = bank_of(f"y{g}{t}{i}", [P, COLS])
+                for half in range(2):
+                    w = (wp[:, half, 2 * COLS * i : 2 * COLS * (i + 1)].bitcast(FP4X4), wp_plane[:, half, cols])
+                    mx(bank[:], h_row_operand[g, half, t], w, half == 0, half == 1)
+                copy_by(engines[i])(out=x[:, cols], in_=bank[:])
+            nc.sync.dma_start(out=y_rows[g, t], in_=x[:])
+
+        def pooled(n, j, engine):
+            bank = bank_of(f"c{n}{j}", [P, COLS])
+            for g in range(2):
+                mx(bank[:], stationary(pool_operand[g], j), h_token_operand[g, n], g == 0, g == 1)
+            x = ring.tile([P, COLS], F32, name=f"c{n}{j}", tag="narrow", bufs=NARROW_BUFS, align_bytes=64)
+            copy_by(engine)(
+                out=x[:].rearrange("p (i u e) -> p i u e", u=2, e=2),
+                in_=bank[:].rearrange("p (u i e) -> p i u e", u=2, e=2),
+            )
+            nc.sync.dma_start(out=c_rows[j][:, COLS * n : COLS * (n + 1)], in_=x[:])
+
+
+        for b in range(2):
+            load_attn(0, b)
         warm(0)
-        turn_pool(0, 0, "s")
-        turn_pool(1, 0, "s")
-        turn_pool(0, 1, "v")
-        turn_pool(1, 1, "s")
+        load_mlp(0, 1)
+        load_weights(0, 0)
+        warm(1)
+        load_mlp(0, 0)
+        load_weights(0, 2)
+        turn_act(0, 0, 0, "vs")
+        load_weights(0, 1)
+        load_attn(1, 0)
+        turn_act(0, 0, 1, "sv")
+        quantize_act(1)
+        sort_act(0, 2, 1, "s")
+        group_weights(0, 0, 320)
+        load_mlp(1, 0)
+        warm(2)
+        quantize_act(0)
+        warm(3)
+        quantize_weights(0, 0)
+        turn_act(0, 1, 1, "ss")
+        warm(4)
+        load_weights(0, 3)
+        warm(5)
+        turn_act(0, 2, 1, "ss")
+        turn_act(0, 2, 0, "vs")
+        load_attn(1, 1)
+        group_weights(0, 2, 320)
+        quantize_act(5)
+        write_stream(0, 0, 0, ALL)
+        group_weights(0, 1, 320)
+        warm(6)
+        load_weights(0, 4)
+        quantize_weights(0, 2)
+        warm(7)
+        turn_act(0, 1, 0, "ss")
+        turn_act(1, 0, 0, "ss")
+        sort_act(1, 1, 0, "s")
+        quantize_weights(0, 1)
+        write_stream(0, 0, 1, ALL)
+        load_weights(0, 5)
+        for k in (2, 4):
+            quantize_act(k)
+        quantize_act_pair(0, 0)
+        for k in range(2):
+            load_weights(1, k)
+        group_weights(0, 3, 384)
+        write_stream(0, 0, 2, ALL)
+        quantize_act(3)
+        turn_act(1, 1, 0, "ss")
+        load_resid(0, 0)
+        quantize_weights(0, 3)
+        turn_act(1, 2, 0, "ss")
+        quantize_act_pair(1, 0)
+        write_stream(1, 0, 0, LOW)
+        for k in range(4, 6):
+            group_weights(0, k, 384)
+        load_weights(1, 2)
+        write_stream(1, 0, 1, LOW)
+        quantize_weights(0, 4)
+        load_weights(1, 3)
+        write_stream(1, 0, 2, LOW)
+        load_weights(1, 4)
+        turn_act(1, 0, 1, "ss")
+        load_weights(1, 5)
+        group_weights(1, 0, 192)
+        quantize_weights(0, 5)
+        write_stream(0, 0, 3, ALL)
+        quantize_act_pair(2, 0)
+        group_weights(1, 1, 128)
+        write_stream(1, 0, 3, LOW)
+        write_stream(0, 0, 4, ALL)
+        quantize_weights(1, 0)
+        load_resid(1, 0)
+        write_stream(0, 0, 5, ALL)
+        write_stream(1, 0, 4, LOW)
+        add_resid(0, 0, 0)
+        group_weights(1, 2, 0)
+        quantize_weights(1, 1)
+        load_mlp(1, 1)
+
+        write_stream(0, 1, 0, ALL)
+        add_resid(0, 0, 1)
+        write_stream(1, 0, 5, LOW)
+        group_weights(1, 3, 256)
+        quantize_weights(1, 2)
+        group_weights(1, 4, 256)
+        quantize_weights(1, 3)
+        write_stream(0, 1, 1, ALL)
+        load_resid(0, 1)
+        for k in range(2):
+            write_stream(1, 1, k, LOW)
+        quantize_act_pair(0, 1)
+        write_stream(0, 1, 2, ALL)
+        write_stream(1, 1, 2, LOW)
+        load_pool_bytes()
+        group_weights(1, 5, 192)
+        quantize_weights(1, 4)
+        add_resid(1, 0, 0)
+        quantize_weights(1, 5)
+        load_pool_scale()
+        write_stream(0, 1, 3, ALL)
+        group_h_tokens(0, 0, 0)
+        write_stream(1, 1, 3, LOW)
+        sort_act(1, 1, 1, "v")
+        write_stream(0, 1, 4, ALL)
+        turn_h(0, 0, 0, "s")
+        turn_h(0, 0, 1, "v")
+        sort_act(1, 2, 1, "s")
+        write_stream(0, 1, 5, ALL)
+        add_resid(0, 1, 0)
+        turn_act(1, 1, 1, "ss")
+        add_resid(0, 1, 1)
+        for k in range(2):
+            write_stream(1, 0, k, HIGH)
+        for b in range(2):
+            turn_h(0, 1, b, "s")
+        quantize_h_tokens(0, 0)
+        turn_act(1, 2, 1, "ss")
+        write_stream(1, 1, 4, LOW)
+        group_h_tokens(0, 1, 0)
+        load_wp()
+        quantize_h_rows(0, 0)
+        quantize_act_pair(1, 1)
+        quantize_h_rows(0, 1)
+        write_stream(1, 1, 0, HIGH)
+        for k in range(2, 4):
+            write_stream(1, 0, k, HIGH)
+        quantize_act_pair(2, 1)
+        write_stream(1, 1, 1, HIGH)
+        write_stream(1, 1, 5, LOW)
+        load_wp_scales()
+        write_stream(1, 0, 4, HIGH)
+        for b in (1, 0):
+            scale_pool(b)
+        write_stream(1, 0, 5, HIGH)
+        write_stream(1, 1, 2, HIGH)
+        load_resid(1, 1)
+        add_resid(1, 0, 1)
+        sort_pool(1, "s")
+
         project(0, 1, "ss")
-        quant_pool(1)
+        write_stream(1, 1, 3, HIGH)
+        add_resid(1, 1, 0)
+        sort_pool(0, "s")
+        write_stream(1, 1, 4, HIGH)
         project(0, 3, "ss")
-        quant_pool(0)
-        add_pair(1, 1, 0)
-        add_pair(1, 1, 1)
-        project(0, 2, "ss")
-        project(0, 0, "ss")
-        quant_hc(0, 1)
-        turn_h(1, 0, 0, "s")
-        turn_h(1, 0, 1, "v")
-        turn_h(1, 1, 1, "v")
-        turn_h(1, 1, 0, "s")
-        pooled(0, 3, "s")
+        group_h_tokens(1, 0, 512)
+        turn_pool(1, "sv")
+        turn_pool(0, "ss")
+        quantize_pool(0)
+        quantize_h_tokens(1, 0)
+        quantize_pool(1)
+        for t in (0, 2):
+            project(0, t, "ss")
+        write_stream(1, 1, 5, HIGH)
+        for j in (2, 1):
+            pooled(0, j, "s")
+        add_resid(1, 1, 1)
         pooled(0, 0, "s")
-        quant_ht(1, 0)
-        pooled(0, 1, "s")
-        quant_ht_pair(1, 1, 1)
-        group_hc(1, 1, 512)
-        quant_ht_pair(1, 1, 0)
-        quant_hc(1, 1)
-        project(1, 3, "ss")
-        project(1, 2, "sv")
-        pooled(0, 2, "s")
-        pooled(1, 1, "v")
-        project(1, 1, "sv")
-        project(1, 0, "sv")
-        pooled(1, 0, "s")
+        quantize_h_tokens(0, 1)
+        group_h_tokens(1, 1, 512)
+        quantize_h_tokens(1, 1)
+        pooled(0, 3, "v")
+        for b in range(2):
+            turn_h(1, 0, b, "s")
+        quantize_h_rows(1, 0)
+        turn_h(1, 1, 1, "s")
+        quantize_h_rows_pair(1, 1, 1)
+        turn_h(1, 1, 0, "v")
         pooled(1, 3, "s")
-        pooled(1, 2, "s")
+        quantize_h_rows_pair(1, 1, 0)
+        for j in (2, 0):
+            pooled(1, j, "s")
+        project(1, 3, "ss")
+        project(1, 1, "sv")
+        project(1, 0, "vs")
+        pooled(1, 1, "v")
+        project(1, 2, "vs")

from contextlib import ExitStack

import concourse.mybir as mybir
from concourse.masks import make_identity

F32 = mybir.dt.float32
BF16 = mybir.dt.bfloat16
U32 = mybir.dt.uint32
I32 = mybir.dt.int32
U8 = mybir.dt.uint8
FP8 = mybir.dt.float8_e4m3fn
FP8X4 = mybir.dt.float8_e4m3fn_x4
FP4X4 = mybir.dt.float4_e2m1fn_x4
ADD = mybir.AluOpType.add
MULT = mybir.AluOpType.mult

P = 128
COLS = 512
TOKENS, SLOTS = 1024, 512
ATTN_WIDTH, MLP_WIDTH, RESIDUAL_WIDTH, PROJECTION_WIDTH = 1024, 2048, 1024, 1024
FLOPS = 2 * TOKENS * RESIDUAL_WIDTH * (ATTN_WIDTH + MLP_WIDTH + PROJECTION_WIDTH + SLOTS)

ATTN_PASSES = ATTN_WIDTH // 512
PASSES = (ATTN_WIDTH + MLP_WIDTH) // 512
ALL, LOW, HIGH = range(4), range(2), range(2, 4)

NARROW_BUFS = 11
MLP_BUFS = 3
SORTED_BUFS = 2
GROUPED_BUFS = 9
COLUMN_CODE_BUFS = 12
BANKS = 8


def tile_two_writer_residual_s8_kernel(
    tc, attn, wo, mlp, wd, resid, wp_words, wp_scales, pool_bytes, pool_scale, out_0, out_1
):
    nc = tc.nc
    with ExitStack() as ctx:
        keep = ctx.enter_context(tc.tile_pool(name="keep", bufs=1))
        ring = ctx.enter_context(tc.tile_pool(name="ring", bufs=2))
        psum = ctx.enter_context(tc.psum_pool(name="psum", bufs=BANKS))

        def kept(label, shape, dtype):
            return keep.tile(shape, dtype, name=label, tag=label, bufs=1, align_bytes=64)

        def grouped(label, columns):
            return ring.tile([P, columns, 4], BF16, name=label, tag="grouped", bufs=GROUPED_BUFS, align_bytes=64)

        def bank_of(label, shape):
            return psum.tile(shape, F32, name=label, tag="bank", bufs=BANKS)

        ident = kept("ident", [P, P], F32)
        wp_plane = kept("wp_plane", [P, 2, PROJECTION_WIDTH], U8)
        zeros = kept("zeros", [P, COLS], BF16)
        nc.vector.memset(zeros[:], 0.0)
        make_identity(nc, ident[:])
        nc.gpsimd.memset(wp_plane[:].rearrange("p g n -> p (g n)").bitcast(I32), 0)

        ctx.enter_context(tc.manual_schedule())

        attn_rows = attn.rearrange("(g p t) k -> g p t k", p=P, t=4)
        mlp_rows = mlp.rearrange("(g p t) k -> g p t k", p=P, t=4)
        resid_rows = resid.rearrange("(g p t) d -> g p t d", p=P, t=4)
        wo_rows = wo.rearrange("(k p j) d -> k p j d", p=P, j=4)
        wd_rows = wd.rearrange("(k p j) d -> k p j d", p=P, j=4)
        y_rows = out_0.rearrange("(g p t) v -> g t p v", p=P, t=4)
        c_rows = out_1.rearrange("(p j) d -> j p d", j=4)

        act_words, act_grouped, act_operand = {}, {}, {}
        weight_raw, weight_grouped, weight_operand = {}, {}, {}
        resid_half, total, h = {}, {}, {}
        h_row_grouped, h_row_operand, h_token_grouped, h_token_operand = {}, {}, {}, {}
        pool_value, pool_words, pool_grouped, pool_operand = {}, {}, {}, {}
        sorted_units = set()

        wp = kept("wp", [P, 2, 2 * PROJECTION_WIDTH], U8)
        pool_raw = kept("pool_raw", [P, 4, TOKENS], U8)
        scale_row = kept("scale_row", [P, TOKENS], F32)

        def load_attn(g, b):
            x = ring.tile([P, 2, ATTN_WIDTH], BF16, name=f"attn{g}{b}", tag="narrow", bufs=NARROW_BUFS, align_bytes=64)
            nc.sync.dma_start(out=x[:], in_=attn_rows[g][:, 2 * b : 2 * b + 2, :])
            act_words[g, 0, b] = x[:].bitcast(F32)

        def load_mlp(g, b):
            x = ring.tile([P, 2, MLP_WIDTH], BF16, name=f"mlp{g}{b}", tag="mlp", bufs=MLP_BUFS, align_bytes=64)
            nc.sync.dma_start(out=x[:], in_=mlp_rows[g][:, 2 * b : 2 * b + 2, :])
            for s in (1, 2):
                act_words[g, s, b] = x[:, :, 1024 * (s - 1) : 1024 * s].bitcast(F32)

        def load_weights(n, k):
            x = ring.tile([P, 4, COLS], BF16, name=f"w{n}{k}", tag="narrow", bufs=NARROW_BUFS, align_bytes=64)
            rows = wo_rows[k] if k < ATTN_PASSES else wd_rows[k - ATTN_PASSES]
            nc.sync.dma_start(out=x[:], in_=rows[:, :, COLS * n : COLS * (n + 1)])
            weight_raw[n, k] = x

        def load_resid(g, n):
            resid_half[g, n] = kept(f"resid{g}{n}", [P, 4, COLS], BF16)
            nc.sync.dma_start(out=resid_half[g, n][:], in_=resid_rows[g][:, :, COLS * n : COLS * (n + 1)])

        def load_wp():
            nc.sync.dma_start(out=wp[:], in_=wp_words.rearrange("g p n -> p g n"))

        def load_wp_scales():
            for q in range(4):
                nc.sync.dma_start(
                    out=wp_plane[32 * q : 32 * q + 4].bitcast(I32),
                    in_=wp_scales[:, 4 * q : 4 * q + 4, :].rearrange("g r n -> r g n").bitcast(I32),
                )

        def load_pool_bytes():
            nc.sync.dma_start(out=pool_raw[:], in_=pool_bytes.rearrange("(p j) m -> p j m", j=4))

        def load_pool_scale():
            nc.sync.dma_start(out=scale_row[:], in_=pool_scale.rearrange("o m -> (o m)").partition_broadcast(P))

        def warm(i):
            bank = bank_of(f"warm{i}", [P, COLS])
            nc.tensor.matmul(bank[:], lhsT=zeros[:, :P], rhs=zeros[:], start=True, stop=True)

        def copy_by(engine):
            return nc.vector.tensor_copy if engine == "v" else nc.scalar.copy

        def sort_words(words, label, engine):
            x = ring.tile([P, 2, 1024], BF16, name=label, tag="sorted", bufs=SORTED_BUFS, align_bytes=64)
            in_order = x[:].bitcast(F32)
            for r in range(2):
                copy_by(engine)(
                    out=in_order[:, r, :].rearrange("p (k u i) -> p k u i", k=2, u=2),
                    in_=words[:, r, :].rearrange("p (k i u) -> p k u i", k=2, u=2),
                )
            return in_order

        def transpose_words(bank, words, i, in_order):
            for r in range(2):
                for u in range(2):
                    if in_order:
                        picked = words[:, r, 256 * i + P * u : 256 * i + P * (u + 1)]
                    else:
                        picked = words[:, r, 256 * i + u : 256 * i + u + 255 : 2]
                    nc.tensor.transpose(bank[:, 2 * r + u, :], picked, ident[:])

        def empty_words(bank, x, first, engine):
            dst = x[:].rearrange("p r j -> p (r j)").bitcast(F32)
            copy_by(engine)(
                out=dst[:, first : first + COLS].rearrange("p (t r u) -> p t r u", t=2, u=2),
                in_=bank[:].rearrange("p (t u) r -> p t r u", u=2),
            )

        def sort_act(g, s, b, engine):
            act_words[g, s, b] = sort_words(act_words[g, s, b], f"sorted{g}{s}{b}", engine)
            sorted_units.add((g, s, b))

        def turn_act(g, s, b, engines):
            for i in range(2):
                k = 2 * s + i
                bank = bank_of(f"turn{g}{k}{b}", [P, 4, P])
                transpose_words(bank, act_words[g, s, b], i, (g, s, b) in sorted_units)
                unit = (g, k) if g == 0 else (g, k, b)
                if unit not in act_grouped:
                    act_grouped[unit] = grouped(f"act{g}{k}{b}", 512 if g == 0 else 256)
                empty_words(bank, act_grouped[unit], COLS * b if g == 0 else 0, engines[i])

        def quantize(label, x, columns, streams=False):
            if streams:
                bufs = COLUMN_CODE_BUFS
                codes = ring.tile([P, columns], U32, name=label + "_codes", tag="codes", bufs=bufs, align_bytes=64)
                plane = ring.tile([P, columns], U8, name=label + "_plane", tag="plane", bufs=bufs, align_bytes=64)
            else:
                codes = kept(label + "_codes", [P, columns], U32)
                plane = kept(label + "_plane", [P, columns], U8)
            nc.vector.quantize_mx(out=codes[:].bitcast(FP8X4), scales=plane[:], in_=x.rearrange("p c j -> p (c j)"))
            return codes, plane

        def stationary(q, t):
            cols = slice(P * t, P * (t + 1))
            return q[0][:, cols].bitcast(FP8X4), q[1][:, cols]

        def moving(q):
            return q[0][:].bitcast(FP8X4), q[1][:]

        def quantize_act(k):
            q = quantize(f"act0{k}", act_grouped[0, k][:], 512)
            for t in ALL:
                act_operand[0, k, t] = stationary(q, t)

        def quantize_act_pair(s, b):
            for k in (2 * s, 2 * s + 1):
                q = quantize(f"act1{k}{b}", act_grouped[1, k, b][:], 256)
                for t in range(2):
                    act_operand[1, k, 2 * b + t] = stationary(q, t)

        def interleave(label, rows, v_cols):
            x = grouped(label, COLS)
            for copy, lo, hi in ((nc.vector.tensor_copy, 0, v_cols), (nc.scalar.copy, v_cols, COLS)):
                if lo < hi:
                    copy(
                        out=x[:, lo:hi, :].rearrange("p (c i) j -> p c j i", i=4),
                        in_=rows[:, :, lo:hi].rearrange("p j (c i) -> p c j i", i=4),
                    )
            return x

        def group_weights(n, k, v_cols):
            weight_grouped[n, k] = interleave(f"w_grouped{n}{k}", weight_raw[n, k], v_cols)

        def quantize_weights(n, k):
            weight_operand[n, k] = moving(quantize(f"w{n}{k}", weight_grouped[n, k][:], COLS, streams=True))

        def mx(out, a, b, start, stop):
            nc.tensor.matmul_mx(out=out, lhsT=a[0], lhsT_scale=a[1], rhs=b[0], rhs_scale=b[1], start=start, stop=stop)

        def write_stream(g, n, k, tiles):
            for t in tiles:
                if k == 0:
                    total[g, n, t] = bank_of(f"total{g}{n}{t}", [P, COLS])
                mx(total[g, n, t][:], act_operand[g, k, t], weight_operand[n, k], k == 0, k == PASSES - 1)

        def add_resid(g, n, b):
            if (g, n) not in h:
                h[g, n] = kept(f"h{g}{n}", [P, 4, COLS], BF16)
            for t in (2 * b, 2 * b + 1):
                nc.vector.tensor_tensor(
                    out=h[g, n][:, t, :].rearrange("p (u i e) -> p u i e", u=2, e=2),
                    in0=total[g, n, t][:].rearrange("p (i u e) -> p u i e", u=2, e=2),
                    in1=resid_half[g, n][:, t, :].rearrange("p (i u e) -> p u i e", u=2, e=2),
                    op=ADD,
                )

        def turn_h(g, n, b, engine):
            bank = bank_of(f"turn_h{g}{n}{b}", [P, 4, P])
            words = h[g, n][:, 2 * b : 2 * b + 2, :].bitcast(F32)
            transpose_words(bank, words, 0, True)
            if (g, n) not in h_row_grouped:
                h_row_grouped[g, n] = grouped(f"h_row{g}{n}", 512)
            empty_words(bank, h_row_grouped[g, n], COLS * b, engine)

        def quantize_h_rows(g, n):
            q = quantize(f"h_row{g}{n}", h_row_grouped[g, n][:], 512)
            for t in ALL:
                h_row_operand[g, n, t] = stationary(q, t)

        def quantize_h_rows_pair(g, n, b):
            q = quantize(f"h_row{g}{n}{b}", h_row_grouped[g, n][:, 256 * b : 256 * (b + 1), :], 256)
            for t in range(2):
                h_row_operand[g, n, 2 * b + t] = stationary(q, t)

        def group_h_tokens(g, n, v_cols):
            h_token_grouped[g, n] = interleave(f"h_token_grouped{g}{n}", h[g, n], v_cols)

        def quantize_h_tokens(g, n):
            h_token_operand[g, n] = moving(quantize(f"h_token{g}{n}", h_token_grouped[g, n][:], COLS, streams=True))

        def scale_pool(b):
            pool_value[b] = ring.tile([P, 2, TOKENS], BF16, name=f"pool{b}", tag="narrow", bufs=NARROW_BUFS, align_bytes=64)
            pool_words[b] = pool_value[b][:].bitcast(F32)
            for r in range(2):
                nc.vector.tensor_tensor(
                    out=pool_value[b][:, r, :],
                    in0=pool_raw[:, 2 * b + r, :].bitcast(FP8),
                    in1=scale_row[:],
                    op=MULT,
                )

        def sort_pool(b, engine):
            pool_words[b] = sort_words(pool_words[b], f"sorted_pool{b}", engine)
            sorted_units.add(b)

        def turn_pool(b, engines):
            for k in range(2):
                bank = bank_of(f"turn_pool{k}{b}", [P, 4, P])
                transpose_words(bank, pool_words[b], k, b in sorted_units)
                if k not in pool_grouped:
                    pool_grouped[k] = grouped(f"pool_grouped{k}", SLOTS)
                empty_words(bank, pool_grouped[k], COLS * b, engines[k])

        def quantize_pool(k):
            pool_operand[k] = quantize(f"pool{k}", pool_grouped[k][:], SLOTS)

        def project(g, t, engines):
            x = ring.tile([P, PROJECTION_WIDTH], F32, name=f"y{g}{t}", tag="narrow", bufs=NARROW_BUFS, align_bytes=64)
            for i in range(2):
                cols = slice(COLS * i, COLS * (i + 1))
                bank = bank_of(f"y{g}{t}{i}", [P, COLS])
                for half in range(2):
                    w = (wp[:, half, 2 * COLS * i : 2 * COLS * (i + 1)].bitcast(FP4X4), wp_plane[:, half, cols])
                    mx(bank[:], h_row_operand[g, half, t], w, half == 0, half == 1)
                copy_by(engines[i])(out=x[:, cols], in_=bank[:])
            nc.sync.dma_start(out=y_rows[g, t], in_=x[:])

        def pooled(n, j, engine):
            bank = bank_of(f"c{n}{j}", [P, COLS])
            for g in range(2):
                mx(bank[:], stationary(pool_operand[g], j), h_token_operand[g, n], g == 0, g == 1)
            x = ring.tile([P, COLS], F32, name=f"c{n}{j}", tag="narrow", bufs=NARROW_BUFS, align_bytes=64)
            copy_by(engine)(
                out=x[:].rearrange("p (i u e) -> p i u e", u=2, e=2),
                in_=bank[:].rearrange("p (u i e) -> p i u e", u=2, e=2),
            )
            nc.sync.dma_start(out=c_rows[j][:, COLS * n : COLS * (n + 1)], in_=x[:])


        for b in range(2):
            load_attn(0, b)
        warm(0)
        load_mlp(0, 1)
        load_weights(0, 0)
        warm(1)
        load_mlp(0, 0)
        load_weights(0, 2)
        turn_act(0, 0, 0, "vs")
        load_weights(0, 1)
        load_attn(1, 0)
        turn_act(0, 0, 1, "sv")
        quantize_act(1)
        sort_act(0, 2, 1, "s")
        group_weights(0, 0, 320)
        load_mlp(1, 0)
        warm(2)
        quantize_act(0)
        warm(3)
        quantize_weights(0, 0)
        turn_act(0, 1, 1, "ss")
        warm(4)
        load_weights(0, 3)
        warm(5)
        turn_act(0, 2, 1, "ss")
        turn_act(0, 2, 0, "vs")
        load_attn(1, 1)
        group_weights(0, 2, 320)
        quantize_act(5)
        write_stream(0, 0, 0, ALL)
        group_weights(0, 1, 320)
        warm(6)
        load_weights(0, 4)
        quantize_weights(0, 2)
        warm(7)
        turn_act(0, 1, 0, "ss")
        turn_act(1, 0, 0, "ss")
        sort_act(1, 1, 0, "s")
        quantize_weights(0, 1)
        write_stream(0, 0, 1, ALL)
        load_weights(0, 5)
        for k in (2, 4):
            quantize_act(k)
        quantize_act_pair(0, 0)
        for k in range(2):
            load_weights(1, k)
        group_weights(0, 3, 384)
        write_stream(0, 0, 2, ALL)
        quantize_act(3)
        turn_act(1, 1, 0, "ss")
        load_resid(0, 0)
        quantize_weights(0, 3)
        turn_act(1, 2, 0, "ss")
        quantize_act_pair(1, 0)
        write_stream(1, 0, 0, LOW)
        for k in range(4, 6):
            group_weights(0, k, 384)
        load_weights(1, 2)
        write_stream(1, 0, 1, LOW)
        quantize_weights(0, 4)
        load_weights(1, 3)
        write_stream(1, 0, 2, LOW)
        load_weights(1, 4)
        turn_act(1, 0, 1, "ss")
        load_weights(1, 5)
        group_weights(1, 0, 192)
        quantize_weights(0, 5)
        write_stream(0, 0, 3, ALL)
        quantize_act_pair(2, 0)
        group_weights(1, 1, 128)
        write_stream(1, 0, 3, LOW)
        write_stream(0, 0, 4, ALL)
        quantize_weights(1, 0)
        load_resid(1, 0)
        write_stream(0, 0, 5, ALL)
        write_stream(1, 0, 4, LOW)
        add_resid(0, 0, 0)
        group_weights(1, 2, 0)
        quantize_weights(1, 1)
        load_mlp(1, 1)

        write_stream(0, 1, 0, ALL)
        add_resid(0, 0, 1)
        write_stream(1, 0, 5, LOW)
        group_weights(1, 3, 256)
        quantize_weights(1, 2)
        group_weights(1, 4, 256)
        quantize_weights(1, 3)
        write_stream(0, 1, 1, ALL)
        load_resid(0, 1)
        for k in range(2):
            write_stream(1, 1, k, LOW)
        quantize_act_pair(0, 1)
        write_stream(0, 1, 2, ALL)
        write_stream(1, 1, 2, LOW)
        load_pool_bytes()
        group_weights(1, 5, 192)
        quantize_weights(1, 4)
        add_resid(1, 0, 0)
        quantize_weights(1, 5)
        load_pool_scale()
        write_stream(0, 1, 3, ALL)
        group_h_tokens(0, 0, 0)
        write_stream(1, 1, 3, LOW)
        sort_act(1, 1, 1, "v")
        write_stream(0, 1, 4, ALL)
        turn_h(0, 0, 0, "s")
        turn_h(0, 0, 1, "v")
        sort_act(1, 2, 1, "s")
        write_stream(0, 1, 5, ALL)
        add_resid(0, 1, 0)
        turn_act(1, 1, 1, "ss")
        add_resid(0, 1, 1)
        for k in range(2):
            write_stream(1, 0, k, HIGH)
        for b in range(2):
            turn_h(0, 1, b, "s")
        quantize_h_tokens(0, 0)
        turn_act(1, 2, 1, "ss")
        write_stream(1, 1, 4, LOW)
        group_h_tokens(0, 1, 0)
        load_wp()
        quantize_h_rows(0, 0)
        quantize_act_pair(1, 1)
        quantize_h_rows(0, 1)
        write_stream(1, 1, 0, HIGH)
        for k in range(2, 4):
            write_stream(1, 0, k, HIGH)
        quantize_act_pair(2, 1)
        write_stream(1, 1, 1, HIGH)
        write_stream(1, 1, 5, LOW)
        load_wp_scales()
        write_stream(1, 0, 4, HIGH)
        for b in (1, 0):
            scale_pool(b)
        write_stream(1, 0, 5, HIGH)
        write_stream(1, 1, 2, HIGH)
        load_resid(1, 1)
        add_resid(1, 0, 1)
        sort_pool(1, "s")

        project(0, 1, "ss")
        write_stream(1, 1, 3, HIGH)
        add_resid(1, 1, 0)
        sort_pool(0, "s")
        write_stream(1, 1, 4, HIGH)
        project(0, 3, "ss")
        group_h_tokens(1, 0, 512)
        turn_pool(1, "sv")
        turn_pool(0, "ss")
        quantize_pool(0)
        quantize_h_tokens(1, 0)
        quantize_pool(1)
        for t in (0, 2):
            project(0, t, "ss")
        write_stream(1, 1, 5, HIGH)
        for j in (2, 1):
            pooled(0, j, "s")
        add_resid(1, 1, 1)
        pooled(0, 0, "s")
        quantize_h_tokens(0, 1)
        group_h_tokens(1, 1, 512)
        quantize_h_tokens(1, 1)
        pooled(0, 3, "v")
        for b in range(2):
            turn_h(1, 0, b, "s")
        quantize_h_rows(1, 0)
        turn_h(1, 1, 1, "s")
        quantize_h_rows_pair(1, 1, 1)
        turn_h(1, 1, 0, "v")
        pooled(1, 3, "s")
        quantize_h_rows_pair(1, 1, 0)
        for j in (2, 0):
            pooled(1, j, "s")
        project(1, 3, "ss")
        project(1, 1, "sv")
        project(1, 0, "vs")
        pooled(1, 1, "v")
        project(1, 2, "vs")
